import numpy as np
import ml_dtypes


def mxq(x, axis, fmt="e4m3"):
    dtype, down = {"e4m3": (ml_dtypes.float8_e4m3fn, 7), "e5m2": (ml_dtypes.float8_e5m2, 14)}[fmt]
    v = np.moveaxis(np.asarray(x, np.float32).astype(ml_dtypes.bfloat16).astype(np.float64), axis, -1)
    blocks = v.reshape(v.shape[:-1] + (-1, 32))
    amax = np.abs(blocks).max(-1, keepdims=True)
    byte = np.maximum(np.where(amax > 0, np.frexp(amax)[1] - 1 + 127, 0) - down, 1)
    scale = np.exp2(byte - 127.0)
    codes = (blocks / scale).astype(np.float32).astype(dtype).astype(np.float64)
    return np.moveaxis((codes * scale).reshape(v.shape), -1, axis)


WIDE = False


def mx_kscale(k):
    if not WIDE:
        return np.ones(k)
    levels = np.array([10, -10, 5, -5, 0])
    if k % 512:
        return np.exp2(np.random.permutation(np.resize(levels, k // 32))).repeat(32)
    a = np.empty((k // 512, 16))
    for p in range(k // 512):
        a[p, :8] = np.random.permutation(np.resize(levels, 8))
        for g in range(8):
            far = levels[np.abs(levels - a[p, g]) >= 10]
            a[p, g + 8] = far[np.random.randint(len(far))]
    return np.exp2(a.ravel()).repeat(32)


BF16 = ml_dtypes.bfloat16


def bf(x):
    return np.asarray(x, np.float32).astype(BF16)


def f64(x):
    return np.asarray(x).astype(np.float64)


E2M1 = np.array([0.0, 0.5, 1.0, 1.5, 2.0, 3.0, 4.0, 6.0, -0.0, -0.5, -1.0, -1.5, -2.0, -3.0, -4.0, -6.0])


def pack_weight(w, fmt):
    k, n = w.shape
    w = f64(bf(w)).reshape(k // 32, 32, n)
    amax = np.abs(w).max(1)
    if fmt == "e4m3":
        byte = np.frexp(amax)[1] - 1 + 127 - 7
    else:
        mant, ex = np.frexp(amax / 6.0)
        byte = np.where(mant > 0.5, ex, ex - 1) + 127
    byte = np.clip(np.where(amax > 0, byte, 1), 1, 254)
    scaled = (w * np.exp2(127.0 - byte)[:, None, :]).reshape(k, n).astype(np.float32)
    by_word = np.ascontiguousarray(scaled.reshape(k // 512, 128, 4, n).transpose(0, 1, 3, 2))
    if fmt == "e4m3":
        words = by_word.astype(ml_dtypes.float8_e4m3fn).view(np.uint8)
    else:
        c = by_word.astype(ml_dtypes.float4_e2m1fn).view(np.uint8) & 0xF
        words = c[..., 0::2] | (c[..., 1::2] << 4)
    return np.ascontiguousarray(words), np.ascontiguousarray(byte.astype(np.uint8).reshape(k // 512, 16, n))


def unpack_weight(words, scales, fmt):
    g, p, n, _ = words.shape
    if fmt == "e4m3":
        vals = np.ascontiguousarray(words).view(ml_dtypes.float8_e4m3fn).astype(np.float64)
    else:
        nib = np.empty((g, p, n, 4), np.uint8)
        nib[..., 0::2] = words & 0xF
        nib[..., 1::2] = words >> 4
        vals = E2M1[nib]
    vals = vals * np.repeat(np.exp2(scales.astype(np.float64) - 127.0), 8, axis=1)[..., None]
    return vals.transpose(0, 1, 3, 2).reshape(g * 512, n)

E4M3FN = np.array([(-1.0 if i & 128 else 1.0) * ((1.0 + (i & 7) / 8.0) * 2.0 ** (((i >> 3) & 15) - 7) if i & 120 else (i & 7) * 2.0 ** -9) for i in range(256)])


def e4m3fn_bytes(y):
    return np.clip(np.asarray(y, np.float64), -448.0, 448.0).astype(np.float32).astype(ml_dtypes.float8_e4m3fn).view(np.uint8)


def e4m3fn_values(b):
    return E4M3FN[b]


NE, NV, NF, C, F = 1536, 1024, 1024, 512, 512


def draw0():
    s0, s2 = mx_kscale(C), mx_kscale(C)
    t0, t2 = mx_kscale(NV), mx_kscale(NF)
    x0 = bf(np.random.standard_normal((NV, C)) * s0[None, :] * t0[:, None])
    x1 = bf(np.random.standard_normal((NE, F)))
    x2 = bf(np.random.standard_normal((NF, C)) * s2[None, :] * t2[:, None])
    inc_down = bf(np.random.standard_normal((NE, NV)) / np.sqrt(NV) / t0[None, :])
    inc_up = bf(np.random.standard_normal((NE, NF)) / np.sqrt(NF) / t2[None, :])
    w0_words, w0_scales = pack_weight(np.random.standard_normal((C, F)) / np.sqrt(C) / s0[:, None], "e4m3")
    w2_words, w2_scales = pack_weight(np.random.standard_normal((C, F)) / np.sqrt(C) / s2[:, None], "e4m3")
    return {
        "x0": x0,
        "x1": x1,
        "x2": x2,
        "inc_down": inc_down,
        "inc_up": inc_up,
        "w0_words": w0_words,
        "w0_scales": w0_scales,
        "w2_words": w2_words,
        "w2_scales": w2_scales,
    }


def incidence_message(incidence, cells, weight_words, weight_scales):
    h = mxq(f64(cells), 1, "e4m3") @ unpack_weight(weight_words, weight_scales, "e4m3")
    return mxq(f64(incidence), 1, "e4m3") @ mxq(h, 0, "e4m3")


def core(x0, x1, x2, inc_down, inc_up, w0_words, w0_scales, w2_words, w2_scales):
    m_down = incidence_message(inc_down, x0, w0_words, w0_scales)
    m_up = incidence_message(inc_up, x2, w2_words, w2_scales)
    z = f64(x1) + m_down + m_up
    return z * (1.0 / (1.0 + np.exp(-z)))


def setup_inputs():
    drawn = draw0()
    full = np.asarray(drawn['inc_up']).astype(np.float64)
    scale = (np.abs(full).reshape(1536, 8, 128).max(axis=(2,)) / 448.0).astype(np.float32)
    given = {}
    for key, value in drawn.items():
        if key == 'inc_up':
            given['inc_up_bytes'] = e4m3fn_bytes(full / np.repeat(scale.astype(np.float64), 128, axis=1))
            given['inc_up_scale'] = scale
        else:
            given[key] = value
    return given


def reference(x0, x1, x2, inc_down, inc_up_bytes, inc_up_scale, w0_words, w0_scales, w2_words, w2_scales):
    return core(x0, x1, x2, inc_down, e4m3fn_values(inc_up_bytes) * np.repeat(inc_up_scale.astype(np.float64), 128, axis=1), w0_words, w0_scales, w2_words, w2_scales)

@@ -1,0 +1,365 @@
+from contextlib import ExitStack
+
+import concourse.mybir as mybir
+from concourse.masks import make_identity
+
+F32 = mybir.dt.float32
+BF16 = mybir.dt.bfloat16
+U32 = mybir.dt.uint32
+I32 = mybir.dt.int32
+U8 = mybir.dt.uint8
+FP8 = mybir.dt.float8_e4m3fn
+FP8X4 = mybir.dt.float8_e4m3fn_x4
+ADD = mybir.AluOpType.add
+MULT = mybir.AluOpType.mult
+SILU = mybir.ActivationFunctionType.Silu
+
+P = 128
+NE, NV, C, F = 1536, 1024, 512, 512
+TILES = NE // P
+PAIRS = TILES // 2
+FLOPS = 2 * 2 * NV * C * F + 2 * 2 * NE * NV * F
+
+
+def tile_simplicialboundarycoboundarymessage_d1p_kernel(
+    tc, x0, x1, x2, inc_down, inc_up_bytes, inc_up_scale, w0_words, w0_scales, w2_words, w2_scales, out
+):
+    nc = tc.nc
+    with ExitStack() as ctx:
+        keep = ctx.enter_context(tc.tile_pool(name="keep", bufs=1))
+        work = ctx.enter_context(tc.tile_pool(name="work", bufs=3))
+        turned = ctx.enter_context(tc.psum_pool(name="turned", bufs=4))
+        sums = ctx.enter_context(tc.psum_pool(name="sums", bufs=4))
+        ctx.enter_context(tc.manual_schedule())
+
+        ident = keep.tile([P, P], F32, name="ident")
+        make_identity(nc, ident[:])
+        idle = keep.tile([P, F], BF16, name="idle")
+        nc.vector.memset(idle[:], 0.0)
+        warm = keep.tile([P, 1], F32, name="warm")
+        nc.vector.memset(warm[:], 0.0)
+        nc.scalar.activation(out=warm[:], in_=warm[:], func=SILU)
+
+        w_scales = keep.tile([P, 2, F], U8, name="w_scales", align_bytes=64)
+        nc.vector.memset(w_scales[:].rearrange("p s n -> p (s n)").bitcast(I32), 0)
+        up_scale = keep.tile([P, TILES, 8], F32, name="up_scale")
+
+        x_raw = [keep.tile([P, 4, C], BF16, name="x_raw%d" % c) for c in range(4)]
+        w_codes = [keep.tile([P, F], U32, name="w_codes%d" % s, align_bytes=64) for s in range(2)]
+        down_raw = [keep.tile([P, 2, NV], BF16, name="down_raw%d" % i) for i in range(PAIRS)]
+        up_raw = [keep.tile([P, 2, NV], U8, name="up_raw%d" % i) for i in range(PAIRS)]
+        edge = [keep.tile([P, 4, F], BF16, name="edge%d" % i) for i in range(3)]
+        down_rows = inc_down.rearrange("(m j) k -> m j k", j=TILES)
+        up_rows = inc_up_bytes.rearrange("(m j) k -> m j k", j=TILES)
+        x1_rows = x1.rearrange("(m j) f -> m j f", j=TILES)
+        out_rows = out.rearrange("(m j) f -> m j f", j=TILES)
+
+        def load_x(c, lo, hi):
+            rows = (x0, x2)[c // 2].rearrange("(g m t) c -> g m t c", m=P, t=4)[c % 2]
+            nc.sync.dma_start(out=x_raw[c][:, lo:hi, :], in_=rows[:, lo:hi, :])
+
+        def load_w(s):
+            words = (w0_words, w2_words)[s][0].rearrange("p n t -> p (n t)").bitcast(I32)
+            nc.sync.dma_start(out=w_codes[s][:].bitcast(I32), in_=words)
+
+        def load_planes(s):
+            for q in range(4):
+                nc.sync.dma_start(
+                    out=w_scales[32 * q : 32 * q + 4, s, :].bitcast(I32),
+                    in_=(w0_scales, w2_scales)[s][0, 4 * q : 4 * q + 4, :].bitcast(I32),
+                )
+
+        def load_scale():
+            nc.sync.dma_start(out=up_scale[:], in_=inc_up_scale.rearrange("(m j) q -> m j q", j=TILES))
+
+        def load_down(i):
+            nc.sync.dma_start(out=down_raw[i][:], in_=down_rows[:, 2 * i : 2 * i + 2, :])
+
+        def load_up(i):
+            nc.sync.dma_start(out=up_raw[i][:], in_=up_rows[:, 2 * i : 2 * i + 2, :])
+
+        def load_edge(i):
+            nc.sync.dma_start(out=edge[i][:], in_=x1_rows[:, 4 * i : 4 * i + 4, :])
+
+        load_x(0, 0, 1)
+        load_x(0, 1, 2)
+        load_x(0, 2, 4)
+        load_x(1, 0, 2)
+        load_x(1, 2, 4)
+        load_planes(0)
+        load_w(0)
+        load_x(2, 0, 4)
+        load_scale()
+        load_up(0)
+        load_w(1)
+        load_x(3, 0, 4)
+        load_planes(1)
+        load_down(0)
+        load_up(1)
+        load_down(1)
+        load_edge(0)
+        load_up(2)
+        load_down(2)
+        load_up(3)
+        load_down(3)
+        load_edge(1)
+        load_up(4)
+        load_down(4)
+        load_up(5)
+        load_down(5)
+        load_edge(2)
+
+        def empty(engine, out_ap, in_ap):
+            if engine == "v":
+                nc.vector.tensor_copy(out=out_ap, in_=in_ap)
+            else:
+                nc.scalar.copy(out=out_ap, in_=in_ap)
+
+        def warm_up(n):
+            bank = sums.tile([P, F], F32, name="acc")
+            for k in range(n):
+                nc.tensor.matmul(bank[:], lhsT=idle[:, :P], rhs=idle[:], start=True, stop=True)
+
+        x_turned = {}
+        x_grouped = {}
+        x_codes = {}
+        x_planes = {}
+
+        def turn_x(c):
+            words = x_raw[c][:].rearrange("m t c -> m (t c)").bitcast(F32)
+            banks = []
+            for half in range(2):
+                bank = turned.tile([P, 2, 256], F32, name="bank")
+                for t in range(2):
+                    base = 256 * (2 * half + t)
+                    for u in range(2):
+                        nc.tensor.transpose(bank[:, u, 128 * t : 128 * t + 128], words[:, base + u : base + 256 : 2], ident[:])
+                banks.append(bank)
+            x_turned[c] = banks
+
+        def empty_x(c, engines):
+            grouped = work.tile([P, 2048], BF16, name="x_grouped", align_bytes=64)
+            view = grouped[:].bitcast(F32).rearrange("p (h x u) -> p h x u", h=2, u=2)
+            for half in range(2):
+                empty(engines[half], view[:, half], x_turned[c][half][:].rearrange("p u x -> p x u"))
+            x_grouped[c] = grouped
+
+        def quantize_x(c):
+            x_codes[c] = work.tile([P, 512], U32, name="x_codes", align_bytes=64)
+            x_planes[c] = work.tile([P, 512], U8, name="x_planes", align_bytes=64)
+            nc.vector.quantize_mx(out=x_codes[c][:].bitcast(FP8X4), scales=x_planes[c][:], in_=x_grouped[c][:])
+
+        h_sums = {}
+        h_grouped = {}
+        h_codes = {}
+        h_planes = {}
+
+        def project(c):
+            banks = []
+            s = c // 2
+            for f in range(4):
+                cols = slice(128 * f, 128 * f + 128)
+                bank = sums.tile([P, 4, 128], F32, name="acc")
+                for t in range(4):
+                    rows = slice(128 * t, 128 * t + 128)
+                    nc.tensor.matmul_mx(
+                        out=bank[:, t, :],
+                        lhsT=x_codes[c][:, rows].bitcast(FP8X4),
+                        lhsT_scale=x_planes[c][:, rows],
+                        rhs=w_codes[s][:, cols].bitcast(FP8X4),
+                        rhs_scale=w_scales[:, s, cols],
+                        start=True,
+                        stop=True,
+                    )
+                banks.append(bank)
+            h_sums[c] = banks
+
+        def empty_h(c, engines):
+            grouped = work.tile([P, 512, 4], BF16, name="h_grouped", align_bytes=64)
+            for f in range(4):
+                empty(engines[f], grouped[:, 128 * f : 128 * f + 128, :], h_sums[c][f][:].rearrange("p t n -> p n t"))
+            h_grouped[c] = grouped
+
+        def quantize_h(c):
+            h_codes[c] = keep.tile([P, 512], U32, name="h_codes%d" % c, align_bytes=64)
+            h_planes[c] = keep.tile([P, 512], U8, name="h_planes%d" % c, align_bytes=64)
+            nc.vector.quantize_mx(
+                out=h_codes[c][:].bitcast(FP8X4), scales=h_planes[c][:], in_=h_grouped[c][:].rearrange("p n t -> p (n t)")
+            )
+
+        wide = {}
+
+        def widen(j):
+            tile = work.tile([P, 2, 2, 128, 2], BF16, name="wide", bufs=4)
+            raw = up_raw[j // 2]
+            for b in range(8):
+                g, q = divmod(b, 4)
+                nc.vector.tensor_scalar(
+                    out=tile[:, g, :, 32 * q : 32 * q + 32, :].rearrange("m u p e -> m p u e"),
+                    in0=raw[:, j % 2, 128 * b : 128 * b + 128].bitcast(FP8).rearrange("m (p u e) -> m p u e", u=2, e=2),
+                    scalar1=up_scale[:, j, b : b + 1],
+                    scalar2=None,
+                    op0=MULT,
+                )
+            wide[j] = tile
+
+        i_turned = {}
+        i_grouped = {}
+        i_codes = {}
+        i_planes = {}
+
+        def turn_down(i):
+            for k in range(2):
+                j = 2 * i + k
+                words = down_raw[i][:, k, :].bitcast(F32)
+                bank = turned.tile([P, 2, 256], F32, name="bank")
+                for g in range(2):
+                    for u in range(2):
+                        nc.tensor.transpose(
+                            bank[:, u, 128 * g : 128 * g + 128], words[:, 256 * g + u : 256 * g + 256 : 2], ident[:]
+                        )
+                i_turned[0, j] = bank
+
+        def turn_up(i):
+            for k in range(2):
+                j = 2 * i + k
+                words = wide[j][:].rearrange("m g u p e -> m (g u p e)").bitcast(F32)
+                bank = turned.tile([P, 2, 256], F32, name="bank")
+                for g in range(2):
+                    for u in range(2):
+                        lo = 256 * g + 128 * u
+                        nc.tensor.transpose(bank[:, u, 128 * g : 128 * g + 128], words[:, lo : lo + 128], ident[:])
+                i_turned[1, j] = bank
+
+        def empty_inc(s, i, engines):
+            grouped = work.tile([P, 2048], BF16, name="i_grouped%d" % s, align_bytes=64)
+            view = grouped[:].bitcast(F32).rearrange("p (h x u) -> p h x u", h=2, u=2)
+            for k in range(2):
+                empty(engines[k], view[:, k], i_turned[s, 2 * i + k][:].rearrange("p u x -> p x u"))
+            i_grouped[s, i] = grouped
+
+        def quantize_inc(s, i):
+            i_codes[s, i] = work.tile([P, 512], U32, name="i_codes%d" % s, align_bytes=64)
+            i_planes[s, i] = work.tile([P, 512], U8, name="i_planes%d" % s, align_bytes=64)
+            nc.vector.quantize_mx(
+                out=i_codes[s, i][:].bitcast(FP8X4), scales=i_planes[s, i][:], in_=i_grouped[s, i][:]
+            )
+
+        z_sums = {}
+
+        def carry(j, lo=0, width=F):
+            i, k = divmod(j, 2)
+            cols = slice(lo, lo + width)
+            bank = sums.tile([P, width], F32, name="acc")
+            for c in range(4):
+                s, g = divmod(c, 2)
+                first = 256 * k + 128 * g
+                nc.tensor.matmul_mx(
+                    out=bank[:],
+                    lhsT=i_codes[s, i][:, first : first + 128].bitcast(FP8X4),
+                    lhsT_scale=i_planes[s, i][:, first : first + 128],
+                    rhs=h_codes[c][:, cols].bitcast(FP8X4),
+                    rhs_scale=h_planes[c][:, cols],
+                    start=(c == 0),
+                    stop=(c == 3),
+                )
+            z_sums[j, lo] = bank
+
+        z_tiles = {}
+
+        def add_edge(j, lo=0, width=F):
+            z = work.tile([P, width], F32, name="z", bufs=5)
+            nc.vector.tensor_tensor(out=z[:], in0=z_sums[j, lo][:], in1=edge[j // 4][:, j % 4, lo : lo + width], op=ADD)
+            z_tiles[j, lo] = z
+
+        def finish(j, lo=0, width=F):
+            result = keep.tile([P, width], F32, name="result%d_%d" % (j, lo))
+            nc.scalar.activation(out=result[:], in_=z_tiles[j, lo][:], func=SILU)
+            nc.sync.dma_start(out=out_rows[:, j, lo : lo + width], in_=result[:])
+
+        warm_up(4)
+        turn_x(0)
+        empty_x(0, "vv")
+        warm_up(2)
+        turn_x(1)
+        quantize_x(0)
+        empty_x(1, "sv")
+        project(0)
+        empty_h(0, "svss")
+        turn_x(2)
+        quantize_x(1)
+        empty_x(2, "ss")
+        widen(1)
+        project(1)
+        widen(0)
+        quantize_x(2)
+        empty_h(1, "sssv")
+        turn_x(3)
+        empty_x(3, "vs")
+        project(2)
+        quantize_h(1)
+        turn_down(0)
+        quantize_h(0)
+        empty_h(2, "svss")
+        empty_inc(0, 0, "ss")
+        turn_up(0)
+        quantize_x(3)
+        empty_inc(1, 0, "ss")
+        widen(2)
+        project(3)
+        quantize_h(2)
+        turn_down(1)
+        quantize_inc(0, 0)
+        widen(3)
+        empty_h(3, "svss")
+        quantize_inc(1, 0)
+        quantize_h(3)
+        empty_inc(0, 1, "ss")
+        turn_up(1)
+        widen(5)
+        quantize_inc(0, 1)
+        empty_inc(1, 1, "ss")
+        widen(4)
+        for i in range(PAIRS):
+            ahead = i + 2 if 0 < i < PAIRS - 2 else None
+            if ahead:
+                turn_down(ahead)
+                turn_up(ahead)
+            if i > 0:
+                finish(2 * i - 2)
+                add_edge(2 * i - 1)
+            if ahead:
+                empty_inc(0, ahead, "ss")
+            if i > 0:
+                finish(2 * i - 1)
+            if ahead:
+                empty_inc(1, ahead, "ss")
+            if i == 0:
+                quantize_inc(1, 1)
+            carry(2 * i)
+            if i + 1 < PAIRS:
+                carry(2 * i + 1)
+            else:
+                for lo in (0, 256):
+                    carry(TILES - 1, lo, 256)
+            if i == 0:
+                turn_down(2)
+                turn_up(2)
+                empty_inc(0, 2, "ss")
+                empty_inc(1, 2, "ss")
+            if i + 3 < PAIRS:
+                widen(2 * i + 6)
+                widen(2 * i + 7)
+            if ahead:
+                quantize_inc(0, ahead)
+            if i == 0:
+                quantize_inc(0, 2)
+            add_edge(2 * i)
+            if ahead:
+                quantize_inc(1, ahead)
+            if i == 0:
+                quantize_inc(1, 2)
+        finish(TILES - 2)
+        for lo in (0, 256):
+            add_edge(TILES - 1, lo, 256)
+            finish(TILES - 1, lo, 256)

@@ -18,7 +18,13 @@ P = 128
 NE, NV, C, F = 1536, 1024, 512, 512
 TILES = NE // P
 PAIRS = TILES // 2
+CHUNKS = 4
 FLOPS = 2 * 2 * NV * C * F + 2 * 2 * NE * NV * F
+TURNED_BANKS = 4
+WARM = 3
+PENG = "sv"
+H3 = "sssv"
+LAST = ((0, 256), (256, 128), (384, 128))
 
 
 def tile_simplicialboundarycoboundarymessage_d1p_kernel(
@@ -28,8 +34,8 @@ def tile_simplicialboundarycoboundarymessage_d1p_kernel(
     with ExitStack() as ctx:
         keep = ctx.enter_context(tc.tile_pool(name="keep", bufs=1))
         work = ctx.enter_context(tc.tile_pool(name="work", bufs=3))
-        turned = ctx.enter_context(tc.psum_pool(name="turned", bufs=4))
-        sums = ctx.enter_context(tc.psum_pool(name="sums", bufs=4))
+        turned = ctx.enter_context(tc.psum_pool(name="turned", bufs=TURNED_BANKS))
+        sums = ctx.enter_context(tc.psum_pool(name="sums", bufs=8 - TURNED_BANKS))
         ctx.enter_context(tc.manual_schedule())
 
         ident = keep.tile([P, P], F32, name="ident")
@@ -40,11 +46,17 @@ def tile_simplicialboundarycoboundarymessage_d1p_kernel(
         nc.vector.memset(warm[:], 0.0)
         nc.scalar.activation(out=warm[:], in_=warm[:], func=SILU)
 
+        def warm_up(n):
+            bank = sums.tile([P, F], F32, name="acc")
+            for k in range(n):
+                nc.tensor.matmul(bank[:], lhsT=idle[:, :P], rhs=idle[:], start=True, stop=True)
+
         w_scales = keep.tile([P, 2, F], U8, name="w_scales", align_bytes=64)
         nc.vector.memset(w_scales[:].rearrange("p s n -> p (s n)").bitcast(I32), 0)
         up_scale = keep.tile([P, TILES, 8], F32, name="up_scale")
 
-        x_raw = [keep.tile([P, 4, C], BF16, name="x_raw%d" % c) for c in range(4)]
+        x_raw = [[keep.tile([P, C], BF16, name="x_raw%d_%d" % (c, t)) for t in range(4)] for c in range(1)]
+        x_raw.extend([keep.tile([P, 4, C], BF16, name="x_raw%d" % c) for c in range(1, CHUNKS)])
         w_codes = [keep.tile([P, F], U32, name="w_codes%d" % s, align_bytes=64) for s in range(2)]
         down_raw = [keep.tile([P, 2, NV], BF16, name="down_raw%d" % i) for i in range(PAIRS)]
         up_raw = [keep.tile([P, 2, NV], U8, name="up_raw%d" % i) for i in range(PAIRS)]
@@ -54,9 +66,17 @@ def tile_simplicialboundarycoboundarymessage_d1p_kernel(
         x1_rows = x1.rearrange("(m j) f -> m j f", j=TILES)
         out_rows = out.rearrange("(m j) f -> m j f", j=TILES)
 
-        def load_x(c, lo, hi):
-            rows = (x0, x2)[c // 2].rearrange("(g m t) c -> g m t c", m=P, t=4)[c % 2]
-            nc.sync.dma_start(out=x_raw[c][:, lo:hi, :], in_=rows[:, lo:hi, :])
+        def x_rows(c):
+            return (x0, x2)[c // 2].rearrange("(g m t) c -> g m t c", m=P, t=4)[c % 2]
+
+        def x_slot(c, t):
+            return x_raw[0][t][:] if c == 0 else x_raw[c][:, t, :]
+
+        def load_x_slot(t):
+            nc.sync.dma_start(out=x_raw[0][t][:], in_=x_rows(0)[:, t, :])
+
+        def load_x(c):
+            nc.sync.dma_start(out=x_raw[c][:], in_=x_rows(c))
 
         def load_w(s):
             words = (w0_words, w2_words)[s][0].rearrange("p n t -> p (n t)").bitcast(I32)
@@ -81,73 +101,59 @@ def tile_simplicialboundarycoboundarymessage_d1p_kernel(
         def load_edge(i):
             nc.sync.dma_start(out=edge[i][:], in_=x1_rows[:, 4 * i : 4 * i + 4, :])
 
-        load_x(0, 0, 1)
-        load_x(0, 1, 2)
-        load_x(0, 2, 4)
-        load_x(1, 0, 2)
-        load_x(1, 2, 4)
+        for t in range(4):
+            load_x_slot(t)
+        load_x(1)
         load_planes(0)
         load_w(0)
-        load_x(2, 0, 4)
+        load_x(2)
         load_scale()
         load_up(0)
         load_w(1)
-        load_x(3, 0, 4)
         load_planes(1)
-        load_down(0)
-        load_up(1)
-        load_down(1)
-        load_edge(0)
-        load_up(2)
-        load_down(2)
-        load_up(3)
-        load_down(3)
-        load_edge(1)
-        load_up(4)
-        load_down(4)
-        load_up(5)
-        load_down(5)
-        load_edge(2)
+        load_x(3)
+        for i in range(PAIRS):
+            load_down(i)
+            if i + 1 < PAIRS:
+                load_up(i + 1)
+            if i % 2 == 1:
+                load_edge(i // 2)
 
-        def empty(engine, out_ap, in_ap):
+        def move(engine, out_ap, in_ap):
             if engine == "v":
                 nc.vector.tensor_copy(out=out_ap, in_=in_ap)
             else:
                 nc.scalar.copy(out=out_ap, in_=in_ap)
-
-        def warm_up(n):
-            bank = sums.tile([P, F], F32, name="acc")
-            for k in range(n):
-                nc.tensor.matmul(bank[:], lhsT=idle[:, :P], rhs=idle[:], start=True, stop=True)
 
         x_turned = {}
         x_grouped = {}
         x_codes = {}
         x_planes = {}
 
-        def turn_x(c):
-            words = x_raw[c][:].rearrange("m t c -> m (t c)").bitcast(F32)
-            banks = []
-            for half in range(2):
-                bank = turned.tile([P, 2, 256], F32, name="bank")
-                for t in range(2):
-                    base = 256 * (2 * half + t)
-                    for u in range(2):
-                        nc.tensor.transpose(bank[:, u, 128 * t : 128 * t + 128], words[:, base + u : base + 256 : 2], ident[:])
-                banks.append(bank)
-            x_turned[c] = banks
+        def turn_x(c, lo, n):
+            bank = turned.tile([P, 2, 128 * n], F32, name="bank")
+            for t in range(n):
+                words = x_slot(c, lo + t).bitcast(F32)
+                for u in range(2):
+                    nc.tensor.transpose(bank[:, u, 128 * t : 128 * t + 128], words[:, u:256:2], ident[:])
+            x_turned[c, lo] = bank
 
-        def empty_x(c, engines):
-            grouped = work.tile([P, 2048], BF16, name="x_grouped", align_bytes=64)
-            view = grouped[:].bitcast(F32).rearrange("p (h x u) -> p h x u", h=2, u=2)
-            for half in range(2):
-                empty(engines[half], view[:, half], x_turned[c][half][:].rearrange("p u x -> p x u"))
-            x_grouped[c] = grouped
+        def empty_x(c, lo, n, engine):
+            if lo == 0:
+                x_grouped[c] = work.tile([P, 2048], BF16, name="x_grouped", align_bytes=64)
+            view = x_grouped[c][:, 512 * lo : 512 * (lo + n)].bitcast(F32).rearrange("p (x u) -> p x u", u=2)
+            move(engine, view, x_turned[c, lo][:].rearrange("p u x -> p x u"))
 
-        def quantize_x(c):
-            x_codes[c] = work.tile([P, 512], U32, name="x_codes", align_bytes=64)
-            x_planes[c] = work.tile([P, 512], U8, name="x_planes", align_bytes=64)
-            nc.vector.quantize_mx(out=x_codes[c][:].bitcast(FP8X4), scales=x_planes[c][:], in_=x_grouped[c][:])
+        def quantize_x(c, lo=0, n=4):
+            if lo == 0:
+                x_codes[c] = work.tile([P, 512], U32, name="x_codes", align_bytes=64)
+                x_planes[c] = work.tile([P, 512], U8, name="x_planes", align_bytes=64)
+            cols = slice(128 * lo, 128 * (lo + n))
+            nc.vector.quantize_mx(
+                out=x_codes[c][:, cols].bitcast(FP8X4),
+                scales=x_planes[c][:, cols],
+                in_=x_grouped[c][:, 512 * lo : 512 * (lo + n)],
+            )
 
         h_sums = {}
         h_grouped = {}
@@ -155,7 +161,6 @@ def tile_simplicialboundarycoboundarymessage_d1p_kernel(
         h_planes = {}
 
         def project(c):
-            banks = []
             s = c // 2
             for f in range(4):
                 cols = slice(128 * f, 128 * f + 128)
@@ -171,14 +176,12 @@ def tile_simplicialboundarycoboundarymessage_d1p_kernel(
                         start=True,
                         stop=True,
                     )
-                banks.append(bank)
-            h_sums[c] = banks
+                h_sums[c, f] = bank
 
-        def empty_h(c, engines):
-            grouped = work.tile([P, 512, 4], BF16, name="h_grouped", align_bytes=64)
-            for f in range(4):
-                empty(engines[f], grouped[:, 128 * f : 128 * f + 128, :], h_sums[c][f][:].rearrange("p t n -> p n t"))
-            h_grouped[c] = grouped
+        def empty_h(c, f, engine):
+            if f == 0:
+                h_grouped[c] = work.tile([P, 512, 4], BF16, name="h_grouped", align_bytes=64)
+            move(engine, h_grouped[c][:, 128 * f : 128 * f + 128, :], h_sums[c, f][:].rearrange("p t n -> p n t"))
 
         def quantize_h(c):
             h_codes[c] = keep.tile([P, 512], U32, name="h_codes%d" % c, align_bytes=64)
@@ -188,6 +191,7 @@ def tile_simplicialboundarycoboundarymessage_d1p_kernel(
             )
 
         wide = {}
+        parted = {}
 
         def widen(j):
             tile = work.tile([P, 2, 2, 128, 2], BF16, name="wide", bufs=4)
@@ -203,72 +207,74 @@ def tile_simplicialboundarycoboundarymessage_d1p_kernel(
                 )
             wide[j] = tile
 
+        def part(j, engine):
+            tile = work.tile([P, 2, 2, 128], F32, name="parted", bufs=4)
+            words = down_raw[j // 2][:, j % 2, :].bitcast(F32)
+            move(engine, tile[:], words.rearrange("m (g p u) -> m g u p", g=2, u=2))
+            parted[j] = tile
+
         i_turned = {}
         i_grouped = {}
         i_codes = {}
         i_planes = {}
 
-        def turn_down(i):
-            for k in range(2):
-                j = 2 * i + k
-                words = down_raw[i][:, k, :].bitcast(F32)
-                bank = turned.tile([P, 2, 256], F32, name="bank")
-                for g in range(2):
-                    for u in range(2):
-                        nc.tensor.transpose(
-                            bank[:, u, 128 * g : 128 * g + 128], words[:, 256 * g + u : 256 * g + 256 : 2], ident[:]
-                        )
-                i_turned[0, j] = bank
+        def turn_down(j):
+            words = down_raw[j // 2][:, j % 2, :].bitcast(F32)
+            bank = turned.tile([P, 2, 256], F32, name="bank")
+            for g in range(2):
+                for u in range(2):
+                    source = parted[j][:, g, u, :] if j in parted else words[:, 256 * g + u : 256 * g + 256 : 2]
+                    nc.tensor.transpose(bank[:, u, 128 * g : 128 * g + 128], source, ident[:])
+            i_turned[0, j] = bank
 
-        def turn_up(i):
-            for k in range(2):
-                j = 2 * i + k
-                words = wide[j][:].rearrange("m g u p e -> m (g u p e)").bitcast(F32)
-                bank = turned.tile([P, 2, 256], F32, name="bank")
-                for g in range(2):
-                    for u in range(2):
-                        lo = 256 * g + 128 * u
-                        nc.tensor.transpose(bank[:, u, 128 * g : 128 * g + 128], words[:, lo : lo + 128], ident[:])
-                i_turned[1, j] = bank
+        def turn_up(j):
+            words = wide[j][:].rearrange("m g u p e -> m (g u p e)").bitcast(F32)
+            bank = turned.tile([P, 2, 256], F32, name="bank")
+            for g in range(2):
+                for u in range(2):
+                    lo = 256 * g + 128 * u
+                    nc.tensor.transpose(bank[:, u, 128 * g : 128 * g + 128], words[:, lo : lo + 128], ident[:])
+            i_turned[1, j] = bank
 
-        def empty_inc(s, i, engines):
-            grouped = work.tile([P, 2048], BF16, name="i_grouped%d" % s, align_bytes=64)
-            view = grouped[:].bitcast(F32).rearrange("p (h x u) -> p h x u", h=2, u=2)
-            for k in range(2):
-                empty(engines[k], view[:, k], i_turned[s, 2 * i + k][:].rearrange("p u x -> p x u"))
-            i_grouped[s, i] = grouped
+        def empty_inc(s, j, engine):
+            if j not in i_grouped:
+                i_grouped[j] = work.tile([P, 2048], BF16, name="i_grouped", bufs=4, align_bytes=64)
+            view = i_grouped[j][:, 1024 * s : 1024 * s + 1024].bitcast(F32).rearrange("p (x u) -> p x u", u=2)
+            move(engine, view, i_turned[s, j][:].rearrange("p u x -> p x u"))
 
-        def quantize_inc(s, i):
-            i_codes[s, i] = work.tile([P, 512], U32, name="i_codes%d" % s, align_bytes=64)
-            i_planes[s, i] = work.tile([P, 512], U8, name="i_planes%d" % s, align_bytes=64)
+        def quantize_inc(j, lo=0, n=2):
+            if j not in i_codes:
+                i_codes[j] = work.tile([P, 512], U32, name="i_codes", bufs=4, align_bytes=64)
+                i_planes[j] = work.tile([P, 512], U8, name="i_planes", bufs=4, align_bytes=64)
+            cols = slice(256 * lo, 256 * (lo + n))
             nc.vector.quantize_mx(
-                out=i_codes[s, i][:].bitcast(FP8X4), scales=i_planes[s, i][:], in_=i_grouped[s, i][:]
+                out=i_codes[j][:, cols].bitcast(FP8X4),
+                scales=i_planes[j][:, cols],
+                in_=i_grouped[j][:, 1024 * lo : 1024 * (lo + n)],
             )
 
         z_sums = {}
 
         def carry(j, lo=0, width=F):
-            i, k = divmod(j, 2)
             cols = slice(lo, lo + width)
             bank = sums.tile([P, width], F32, name="acc")
-            for c in range(4):
-                s, g = divmod(c, 2)
-                first = 256 * k + 128 * g
+            for c in range(CHUNKS):
+                rows = slice(128 * c, 128 * c + 128)
                 nc.tensor.matmul_mx(
                     out=bank[:],
-                    lhsT=i_codes[s, i][:, first : first + 128].bitcast(FP8X4),
-                    lhsT_scale=i_planes[s, i][:, first : first + 128],
+                    lhsT=i_codes[j][:, rows].bitcast(FP8X4),
+                    lhsT_scale=i_planes[j][:, rows],
                     rhs=h_codes[c][:, cols].bitcast(FP8X4),
                     rhs_scale=h_planes[c][:, cols],
                     start=(c == 0),
-                    stop=(c == 3),
+                    stop=(c == CHUNKS - 1),
                 )
             z_sums[j, lo] = bank
 
         z_tiles = {}
 
         def add_edge(j, lo=0, width=F):
-            z = work.tile([P, width], F32, name="z", bufs=5)
+            z = work.tile([P, width], F32, name="z", bufs=4)
             nc.vector.tensor_tensor(out=z[:], in0=z_sums[j, lo][:], in1=edge[j // 4][:, j % 4, lo : lo + width], op=ADD)
             z_tiles[j, lo] = z
 
@@ -277,89 +283,73 @@ def tile_simplicialboundarycoboundarymessage_d1p_kernel(
             nc.scalar.activation(out=result[:], in_=z_tiles[j, lo][:], func=SILU)
             nc.sync.dma_start(out=out_rows[:, j, lo : lo + width], in_=result[:])
 
-        warm_up(4)
-        turn_x(0)
-        empty_x(0, "vv")
+        warm_up(WARM)
+        first = ((0, 2), (2, 1), (3, 1))
+        for lo, n in first:
+            turn_x(0, lo, n)
+        empty_x(0, 0, 2, "v")
+        empty_x(0, 2, 1, "s")
+        quantize_x(0, 0, 2)
+        empty_x(0, 3, 1, "s")
+        quantize_x(0, 2, 1)
+        quantize_x(0, 3, 1)
         warm_up(2)
-        turn_x(1)
-        quantize_x(0)
-        empty_x(1, "sv")
-        project(0)
-        empty_h(0, "svss")
-        turn_x(2)
-        quantize_x(1)
-        empty_x(2, "ss")
-        widen(1)
-        project(1)
-        widen(0)
-        quantize_x(2)
-        empty_h(1, "sssv")
-        turn_x(3)
-        empty_x(3, "vs")
-        project(2)
-        quantize_h(1)
+        for c in range(CHUNKS - 1):
+            turn_x(c + 1, 0, 2)
+            turn_x(c + 1, 2, 2)
+            empty_x(c + 1, 0, 2, "s")
+            empty_x(c + 1, 2, 2, "v")
+            project(c)
+            for f in range(4):
+                if c == 0 and f == 1:
+                    empty_h(c, f, "v")
+                else:
+                    empty_h(c, f, "s")
+            if c > 0:
+                quantize_h(c - 1)
+            quantize_x(c + 1)
+            widen(c)
+        last = CHUNKS - 1
         turn_down(0)
-        quantize_h(0)
-        empty_h(2, "svss")
-        empty_inc(0, 0, "ss")
         turn_up(0)
-        quantize_x(3)
-        empty_inc(1, 0, "ss")
-        widen(2)
-        project(3)
-        quantize_h(2)
+        project(last)
+        empty_inc(1, 0, "v")
+        empty_inc(0, 0, "s")
+        quantize_h(last - 1)
+        quantize_inc(0)
+        for f in range(4):
+            empty_h(last, f, H3[f])
         turn_down(1)
-        quantize_inc(0, 0)
-        widen(3)
-        empty_h(3, "svss")
-        quantize_inc(1, 0)
-        quantize_h(3)
-        empty_inc(0, 1, "ss")
         turn_up(1)
-        widen(5)
-        quantize_inc(0, 1)
-        empty_inc(1, 1, "ss")
-        widen(4)
-        for i in range(PAIRS):
-            ahead = i + 2 if 0 < i < PAIRS - 2 else None
-            if ahead:
-                turn_down(ahead)
-                turn_up(ahead)
-            if i > 0:
-                finish(2 * i - 2)
-                add_edge(2 * i - 1)
-            if ahead:
-                empty_inc(0, ahead, "ss")
-            if i > 0:
-                finish(2 * i - 1)
-            if ahead:
-                empty_inc(1, ahead, "ss")
-            if i == 0:
-                quantize_inc(1, 1)
-            carry(2 * i)
-            if i + 1 < PAIRS:
-                carry(2 * i + 1)
+        quantize_h(last)
+        empty_inc(0, 1, "s")
+        empty_inc(1, 1, "s")
+        for j in range(TILES):
+            a = j + 2
+            if a < TILES:
+                turn_down(a)
+                turn_up(a)
+            if j + 1 < TILES:
+                carry(j)
             else:
-                for lo in (0, 256):
-                    carry(TILES - 1, lo, 256)
-            if i == 0:
-                turn_down(2)
-                turn_up(2)
-                empty_inc(0, 2, "ss")
-                empty_inc(1, 2, "ss")
-            if i + 3 < PAIRS:
-                widen(2 * i + 6)
-                widen(2 * i + 7)
-            if ahead:
-                quantize_inc(0, ahead)
-            if i == 0:
-                quantize_inc(0, 2)
-            add_edge(2 * i)
-            if ahead:
-                quantize_inc(1, ahead)
-            if i == 0:
-                quantize_inc(1, 2)
-        finish(TILES - 2)
-        for lo in (0, 256):
-            add_edge(TILES - 1, lo, 256)
-            finish(TILES - 1, lo, 256)
+                for lo, width in LAST:
+                    carry(j, lo, width)
+            if a + 1 < TILES:
+                if PENG[a % 2] != "n":
+                    part(a + 1, PENG[a % 2])
+                widen(a + 1)
+            early = j == 0 or a == TILES
+            if early:
+                quantize_inc(a - 1)
+            if j > 0:
+                add_edge(j - 1)
+            if a < TILES:
+                empty_inc(0, a, "s")
+                empty_inc(1, a, "s")
+            if j > 0:
+                finish(j - 1)
+            if a - 1 < TILES and not early:
+                quantize_inc(a - 1)
+        for lo, width in LAST:
+            add_edge(TILES - 1, lo, width)
+            finish(TILES - 1, lo, width)

@@ -22,8 +22,10 @@ CHUNKS = 4
 FLOPS = 2 * 2 * NV * C * F + 2 * 2 * NE * NV * F
 TURNED_BANKS = 4
 WARM = 3
+X_PIECES = (((0,1),(1,1),(2,1),(3,1)),((0,2),(2,2)),((0,4),),((0,4),))
 PENG = "sv"
 H3 = "sssv"
+HALVED = 9
 LAST = ((0, 256), (256, 128), (384, 128))
 
 
@@ -55,8 +57,12 @@ def tile_simplicialboundarycoboundarymessage_d1p_kernel(
         nc.vector.memset(w_scales[:].rearrange("p s n -> p (s n)").bitcast(I32), 0)
         up_scale = keep.tile([P, TILES, 8], F32, name="up_scale")
 
-        x_raw = [[keep.tile([P, C], BF16, name="x_raw%d_%d" % (c, t)) for t in range(4)] for c in range(1)]
-        x_raw.extend([keep.tile([P, 4, C], BF16, name="x_raw%d" % c) for c in range(1, CHUNKS)])
+        x_raw = {}
+        for c in range(CHUNKS):
+            for lo, n in X_PIECES[c]:
+                piece = keep.tile([P, n, C], BF16, name="x_raw%d_%d" % (c, lo))
+                for t in range(n):
+                    x_raw[c, lo + t] = (piece, t)
         w_codes = [keep.tile([P, F], U32, name="w_codes%d" % s, align_bytes=64) for s in range(2)]
         down_raw = [keep.tile([P, 2, NV], BF16, name="down_raw%d" % i) for i in range(PAIRS)]
         up_raw = [keep.tile([P, 2, NV], U8, name="up_raw%d" % i) for i in range(PAIRS)]
@@ -70,13 +76,12 @@ def tile_simplicialboundarycoboundarymessage_d1p_kernel(
             return (x0, x2)[c // 2].rearrange("(g m t) c -> g m t c", m=P, t=4)[c % 2]
 
         def x_slot(c, t):
-            return x_raw[0][t][:] if c == 0 else x_raw[c][:, t, :]
-
-        def load_x_slot(t):
-            nc.sync.dma_start(out=x_raw[0][t][:], in_=x_rows(0)[:, t, :])
+            piece, row = x_raw[c, t]
+            return piece[:, row, :]
 
         def load_x(c):
-            nc.sync.dma_start(out=x_raw[c][:], in_=x_rows(c))
+            for lo, n in X_PIECES[c]:
+                nc.sync.dma_start(out=x_raw[c, lo][0][:], in_=x_rows(c)[:, lo : lo + n, :])
 
         def load_w(s):
             words = (w0_words, w2_words)[s][0].rearrange("p n t -> p (n t)").bitcast(I32)
@@ -101,17 +106,16 @@ def tile_simplicialboundarycoboundarymessage_d1p_kernel(
         def load_edge(i):
             nc.sync.dma_start(out=edge[i][:], in_=x1_rows[:, 4 * i : 4 * i + 4, :])
 
-        for t in range(4):
-            load_x_slot(t)
+        load_x(0)
         load_x(1)
         load_planes(0)
         load_w(0)
         load_x(2)
         load_scale()
         load_up(0)
-        load_w(1)
-        load_planes(1)
         load_x(3)
+        load_planes(1)
+        load_w(1)
         for i in range(PAIRS):
             load_down(i)
             if i + 1 < PAIRS:
@@ -257,7 +261,10 @@ def tile_simplicialboundarycoboundarymessage_d1p_kernel(
 
         def carry(j, lo=0, width=F):
             cols = slice(lo, lo + width)
-            bank = sums.tile([P, width], F32, name="acc")
+            if j == TILES - 1:
+                bank = turned.tile([P, width], F32, name="bank")
+            else:
+                bank = sums.tile([P, width], F32, name="acc")
             for c in range(CHUNKS):
                 rows = slice(128 * c, 128 * c + 128)
                 nc.tensor.matmul_mx(
@@ -274,7 +281,7 @@ def tile_simplicialboundarycoboundarymessage_d1p_kernel(
         z_tiles = {}
 
         def add_edge(j, lo=0, width=F):
-            z = work.tile([P, width], F32, name="z", bufs=4)
+            z = work.tile([P, width], F32, name="z", bufs=6)
             nc.vector.tensor_tensor(out=z[:], in0=z_sums[j, lo][:], in1=edge[j // 4][:, j % 4, lo : lo + width], op=ADD)
             z_tiles[j, lo] = z
 
@@ -282,6 +289,11 @@ def tile_simplicialboundarycoboundarymessage_d1p_kernel(
             result = keep.tile([P, width], F32, name="result%d_%d" % (j, lo))
             nc.scalar.activation(out=result[:], in_=z_tiles[j, lo][:], func=SILU)
             nc.sync.dma_start(out=out_rows[:, j, lo : lo + width], in_=result[:])
+
+        def parts(j):
+            if j == TILES - 1:
+                return LAST
+            return ((0, 256), (256, 256)) if j >= HALVED else ((0, F),)
 
         warm_up(WARM)
         first = ((0, 2), (2, 1), (3, 1))
@@ -329,27 +341,29 @@ def tile_simplicialboundarycoboundarymessage_d1p_kernel(
             if a < TILES:
                 turn_down(a)
                 turn_up(a)
-            if j + 1 < TILES:
-                carry(j)
-            else:
-                for lo, width in LAST:
-                    carry(j, lo, width)
+            for lo, width in parts(j):
+                carry(j, lo, width)
             if a + 1 < TILES:
                 if PENG[a % 2] != "n":
                     part(a + 1, PENG[a % 2])
                 widen(a + 1)
             early = j == 0 or a == TILES
-            if early:
-                quantize_inc(a - 1)
+            if j == 0:
+                quantize_inc(1)
+            if a == TILES:
+                for s in range(2):
+                    quantize_inc(a - 1, s, 1)
             if j > 0:
-                add_edge(j - 1)
+                for lo, width in parts(j - 1):
+                    add_edge(j - 1, lo, width)
             if a < TILES:
                 empty_inc(0, a, "s")
                 empty_inc(1, a, "s")
             if j > 0:
-                finish(j - 1)
+                for lo, width in parts(j - 1):
+                    finish(j - 1, lo, width)
             if a - 1 < TILES and not early:
                 quantize_inc(a - 1)
-        for lo, width in LAST:
+        for lo, width in parts(TILES - 1):
             add_edge(TILES - 1, lo, width)
             finish(TILES - 1, lo, width)

@@ -22,8 +22,7 @@ CHUNKS = 4
 FLOPS = 2 * 2 * NV * C * F + 2 * 2 * NE * NV * F
 TURNED_BANKS = 4
 WARM = 3
-X_PIECES = (((0,1),(1,1),(2,1),(3,1)),((0,2),(2,2)),((0,4),),((0,4),))
-PENG = "sv"
+X_PIECES = (((0, 1), (1, 1), (2, 1), (3, 1)), ((0, 2), (2, 2)), ((0, 4),), ((0, 4),))
 H3 = "sssv"
 HALVED = 9
 LAST = ((0, 256), (256, 128), (384, 128))
@@ -331,39 +330,57 @@ def tile_simplicialboundarycoboundarymessage_d1p_kernel(
         quantize_inc(0)
         for f in range(4):
             empty_h(last, f, H3[f])
-        turn_down(1)
-        turn_up(1)
-        quantize_h(last)
-        empty_inc(0, 1, "s")
-        empty_inc(1, 1, "s")
-        for j in range(TILES):
-            a = j + 2
-            if a < TILES:
-                turn_down(a)
-                turn_up(a)
+        def carry_all(j):
             for lo, width in parts(j):
                 carry(j, lo, width)
-            if a + 1 < TILES:
-                if PENG[a % 2] != "n":
-                    part(a + 1, PENG[a % 2])
-                widen(a + 1)
-            early = j == 0 or a == TILES
-            if j == 0:
-                quantize_inc(1)
-            if a == TILES:
-                for s in range(2):
-                    quantize_inc(a - 1, s, 1)
-            if j > 0:
-                for lo, width in parts(j - 1):
-                    add_edge(j - 1, lo, width)
-            if a < TILES:
-                empty_inc(0, a, "s")
-                empty_inc(1, a, "s")
-            if j > 0:
-                for lo, width in parts(j - 1):
-                    finish(j - 1, lo, width)
-            if a - 1 < TILES and not early:
+
+        def add_all(j):
+            for lo, width in parts(j):
+                add_edge(j, lo, width)
+
+        def finish_all(j):
+            for lo, width in parts(j):
+                finish(j, lo, width)
+
+        for i in range(PAIRS):
+            a, b = 2 * i + 1, 2 * i + 2
+            now = [j for j in (a, b) if j < TILES]
+            for j in now:
+                turn_down(j)
+            for j in now:
+                turn_up(j)
+            if i == 0:
+                part(a + 2, "v")
+                quantize_h(last)
+            else:
+                carry_all(a - 2)
+                if i > 1:
+                    add_all(a - 4)
+                add_all(a - 3)
                 quantize_inc(a - 1)
-        for lo, width in parts(TILES - 1):
-            add_edge(TILES - 1, lo, width)
-            finish(TILES - 1, lo, width)
+            carry_all(a - 1)
+            for s in range(2):
+                for j in now:
+                    empty_inc(s, j, "s")
+            if a + 2 < TILES:
+                if i > 0:
+                    part(a + 2, "v" if b + 2 < TILES else "s")
+                widen(a + 2)
+            if b + 2 < TILES:
+                if i > 0:
+                    part(b + 2, "s")
+                widen(b + 2)
+            if i > 1:
+                finish_all(a - 4)
+            if i > 0:
+                finish_all(a - 3)
+            if b < TILES:
+                quantize_inc(a)
+            else:
+                for s in range(2):
+                    quantize_inc(a, s, 1)
+        carry_all(TILES - 1)
+        for j in (TILES - 3, TILES - 2, TILES - 1):
+            for lo, width in parts(j):
+                add_edge(j, lo, width)
+                finish(j, lo, width)

@@ -22,8 +22,10 @@ CHUNKS = 4
 FLOPS = 2 * 2 * NV * C * F + 2 * 2 * NE * NV * F
 TURNED_BANKS = 4
 WARM = 3
-X_PIECES = (((0, 1), (1, 1), (2, 1), (3, 1)), ((0, 2), (2, 2)), ((0, 4),), ((0, 4),))
+X_PIECES = (((0, 2), (2, 2)), ((0, 2), (2, 2)), ((0, 4),), ((0, 4),))
 H3 = "sssv"
+PA = "vvvvs"
+PB = "nsss"
 HALVED = 9
 LAST = ((0, 256), (256, 128), (384, 128))
 
@@ -43,15 +45,6 @@ def tile_simplicialboundarycoboundarymessage_d1p_kernel(
         make_identity(nc, ident[:])
         idle = keep.tile([P, F], BF16, name="idle")
         nc.vector.memset(idle[:], 0.0)
-        warm = keep.tile([P, 1], F32, name="warm")
-        nc.vector.memset(warm[:], 0.0)
-        nc.scalar.activation(out=warm[:], in_=warm[:], func=SILU)
-
-        def warm_up(n):
-            bank = sums.tile([P, F], F32, name="acc")
-            for k in range(n):
-                nc.tensor.matmul(bank[:], lhsT=idle[:, :P], rhs=idle[:], start=True, stop=True)
-
         w_scales = keep.tile([P, 2, F], U8, name="w_scales", align_bytes=64)
         nc.vector.memset(w_scales[:].rearrange("p s n -> p (s n)").bitcast(I32), 0)
         up_scale = keep.tile([P, TILES, 8], F32, name="up_scale")
@@ -86,15 +79,15 @@ def tile_simplicialboundarycoboundarymessage_d1p_kernel(
             words = (w0_words, w2_words)[s][0].rearrange("p n t -> p (n t)").bitcast(I32)
             nc.sync.dma_start(out=w_codes[s][:].bitcast(I32), in_=words)
 
-        def load_planes(s):
+        def load_planes(s, queue):
             for q in range(4):
-                nc.sync.dma_start(
+                queue.dma_start(
                     out=w_scales[32 * q : 32 * q + 4, s, :].bitcast(I32),
                     in_=(w0_scales, w2_scales)[s][0, 4 * q : 4 * q + 4, :].bitcast(I32),
                 )
 
-        def load_scale():
-            nc.sync.dma_start(out=up_scale[:], in_=inc_up_scale.rearrange("(m j) q -> m j q", j=TILES))
+        def load_scale(queue):
+            queue.dma_start(out=up_scale[:], in_=inc_up_scale.rearrange("(m j) q -> m j q", j=TILES))
 
         def load_down(i):
             nc.sync.dma_start(out=down_raw[i][:], in_=down_rows[:, 2 * i : 2 * i + 2, :])
@@ -105,15 +98,15 @@ def tile_simplicialboundarycoboundarymessage_d1p_kernel(
         def load_edge(i):
             nc.sync.dma_start(out=edge[i][:], in_=x1_rows[:, 4 * i : 4 * i + 4, :])
 
+        load_planes(0, nc.scalar)
         load_x(0)
         load_x(1)
-        load_planes(0)
         load_w(0)
         load_x(2)
-        load_scale()
+        load_scale(nc.sync)
         load_up(0)
         load_x(3)
-        load_planes(1)
+        load_planes(1, nc.sync)
         load_w(1)
         for i in range(PAIRS):
             load_down(i)
@@ -121,6 +114,16 @@ def tile_simplicialboundarycoboundarymessage_d1p_kernel(
                 load_up(i + 1)
             if i % 2 == 1:
                 load_edge(i // 2)
+
+        warm = keep.tile([P, 1], F32, name="warm")
+        nc.vector.memset(warm[:], 0.0)
+        nc.scalar.activation(out=warm[:], in_=warm[:], func=SILU)
+
+        def warm_up(n):
+            bank = sums.tile([P, F], F32, name="acc")
+            for k in range(n):
+                nc.tensor.matmul(bank[:], lhsT=idle[:, :P], rhs=idle[:], start=True, stop=True)
+
 
         def move(engine, out_ap, in_ap):
             if engine == "v":
@@ -350,7 +353,8 @@ def tile_simplicialboundarycoboundarymessage_d1p_kernel(
             for j in now:
                 turn_up(j)
             if i == 0:
-                part(a + 2, "v")
+                if PA[0] != "n":
+                    part(a + 2, PA[0])
                 quantize_h(last)
             else:
                 carry_all(a - 2)
@@ -363,12 +367,12 @@ def tile_simplicialboundarycoboundarymessage_d1p_kernel(
                 for j in now:
                     empty_inc(s, j, "s")
             if a + 2 < TILES:
-                if i > 0:
-                    part(a + 2, "v" if b + 2 < TILES else "s")
+                if i > 0 and PA[i] != "n":
+                    part(a + 2, PA[i])
                 widen(a + 2)
             if b + 2 < TILES:
-                if i > 0:
-                    part(b + 2, "s")
+                if PB[i] != "n":
+                    part(b + 2, PB[i])
                 widen(b + 2)
             if i > 1:
                 finish_all(a - 4)

@@ -24,7 +24,7 @@ TURNED_BANKS = 4
 WARM = 3
 X_PIECES = (((0, 2), (2, 2)), ((0, 2), (2, 2)), ((0, 4),), ((0, 4),))
 H3 = "sssv"
-PA = "vvvvs"
+PA = "vnnnv"
 PB = "nsss"
 HALVED = 9
 LAST = ((0, 256), (256, 128), (384, 128))

@@ -24,8 +24,10 @@ TURNED_BANKS = 4
 WARM = 3
 X_PIECES = (((0, 2), (2, 2)), ((0, 2), (2, 2)), ((0, 4),), ((0, 4),))
 H3 = "sssv"
-PA = "vnnnv"
-PB = "nsss"
+PENG = "nnnnnnsnsnsv"
+COUNTS = (1,2,1,2,1)
+SILUS = (0,1,2,2,2)
+QLAST = 2
 HALVED = 9
 LAST = ((0, 256), (256, 128), (384, 128))
 
@@ -45,7 +47,7 @@ def tile_simplicialboundarycoboundarymessage_d1p_kernel(
         make_identity(nc, ident[:])
         idle = keep.tile([P, F], BF16, name="idle")
         nc.vector.memset(idle[:], 0.0)
-        w_scales = keep.tile([P, 2, F], U8, name="w_scales", align_bytes=64)
+        w_scales = keep.tile([P, 2, F], U8, name="w_scales", align_bytes=256)
         nc.vector.memset(w_scales[:].rearrange("p s n -> p (s n)").bitcast(I32), 0)
         up_scale = keep.tile([P, TILES, 8], F32, name="up_scale")
 
@@ -55,7 +57,7 @@ def tile_simplicialboundarycoboundarymessage_d1p_kernel(
                 piece = keep.tile([P, n, C], BF16, name="x_raw%d_%d" % (c, lo))
                 for t in range(n):
                     x_raw[c, lo + t] = (piece, t)
-        w_codes = [keep.tile([P, F], U32, name="w_codes%d" % s, align_bytes=64) for s in range(2)]
+        w_codes = [keep.tile([P, F], U32, name="w_codes%d" % s, align_bytes=256) for s in range(2)]
         down_raw = [keep.tile([P, 2, NV], BF16, name="down_raw%d" % i) for i in range(PAIRS)]
         up_raw = [keep.tile([P, 2, NV], U8, name="up_raw%d" % i) for i in range(PAIRS)]
         edge = [keep.tile([P, 4, F], BF16, name="edge%d" % i) for i in range(3)]
@@ -146,14 +148,14 @@ def tile_simplicialboundarycoboundarymessage_d1p_kernel(
 
         def empty_x(c, lo, n, engine):
             if lo == 0:
-                x_grouped[c] = work.tile([P, 2048], BF16, name="x_grouped", align_bytes=64)
+                x_grouped[c] = work.tile([P, 2048], BF16, name="x_grouped", align_bytes=256)
             view = x_grouped[c][:, 512 * lo : 512 * (lo + n)].bitcast(F32).rearrange("p (x u) -> p x u", u=2)
             move(engine, view, x_turned[c, lo][:].rearrange("p u x -> p x u"))
 
         def quantize_x(c, lo=0, n=4):
             if lo == 0:
-                x_codes[c] = work.tile([P, 512], U32, name="x_codes", align_bytes=64)
-                x_planes[c] = work.tile([P, 512], U8, name="x_planes", align_bytes=64)
+                x_codes[c] = work.tile([P, 512], U32, name="x_codes", align_bytes=256)
+                x_planes[c] = work.tile([P, 512], U8, name="x_planes", align_bytes=256)
             cols = slice(128 * lo, 128 * (lo + n))
             nc.vector.quantize_mx(
                 out=x_codes[c][:, cols].bitcast(FP8X4),
@@ -186,12 +188,12 @@ def tile_simplicialboundarycoboundarymessage_d1p_kernel(
 
         def empty_h(c, f, engine):
             if f == 0:
-                h_grouped[c] = work.tile([P, 512, 4], BF16, name="h_grouped", align_bytes=64)
+                h_grouped[c] = work.tile([P, 512, 4], BF16, name="h_grouped", align_bytes=256)
             move(engine, h_grouped[c][:, 128 * f : 128 * f + 128, :], h_sums[c, f][:].rearrange("p t n -> p n t"))
 
         def quantize_h(c):
-            h_codes[c] = keep.tile([P, 512], U32, name="h_codes%d" % c, align_bytes=64)
-            h_planes[c] = keep.tile([P, 512], U8, name="h_planes%d" % c, align_bytes=64)
+            h_codes[c] = keep.tile([P, 512], U32, name="h_codes%d" % c, align_bytes=256)
+            h_planes[c] = keep.tile([P, 512], U8, name="h_planes%d" % c, align_bytes=256)
             nc.vector.quantize_mx(
                 out=h_codes[c][:].bitcast(FP8X4), scales=h_planes[c][:], in_=h_grouped[c][:].rearrange("p n t -> p (n t)")
             )
@@ -244,14 +246,14 @@ def tile_simplicialboundarycoboundarymessage_d1p_kernel(
 
         def empty_inc(s, j, engine):
             if j not in i_grouped:
-                i_grouped[j] = work.tile([P, 2048], BF16, name="i_grouped", bufs=4, align_bytes=64)
+                i_grouped[j] = work.tile([P, 2048], BF16, name="i_grouped", bufs=4, align_bytes=256)
             view = i_grouped[j][:, 1024 * s : 1024 * s + 1024].bitcast(F32).rearrange("p (x u) -> p x u", u=2)
             move(engine, view, i_turned[s, j][:].rearrange("p u x -> p x u"))
 
         def quantize_inc(j, lo=0, n=2):
             if j not in i_codes:
-                i_codes[j] = work.tile([P, 512], U32, name="i_codes", bufs=4, align_bytes=64)
-                i_planes[j] = work.tile([P, 512], U8, name="i_planes", bufs=4, align_bytes=64)
+                i_codes[j] = work.tile([P, 512], U32, name="i_codes", bufs=7, align_bytes=256)
+                i_planes[j] = work.tile([P, 512], U8, name="i_planes", bufs=7, align_bytes=256)
             cols = slice(256 * lo, 256 * (lo + n))
             nc.vector.quantize_mx(
                 out=i_codes[j][:, cols].bitcast(FP8X4),
@@ -283,7 +285,7 @@ def tile_simplicialboundarycoboundarymessage_d1p_kernel(
         z_tiles = {}
 
         def add_edge(j, lo=0, width=F):
-            z = work.tile([P, width], F32, name="z", bufs=6)
+            z = work.tile([P, width], F32, name="z", bufs=12)
             nc.vector.tensor_tensor(out=z[:], in0=z_sums[j, lo][:], in1=edge[j // 4][:, j % 4, lo : lo + width], op=ADD)
             z_tiles[j, lo] = z
 
@@ -345,46 +347,56 @@ def tile_simplicialboundarycoboundarymessage_d1p_kernel(
             for lo, width in parts(j):
                 finish(j, lo, width)
 
+        carried = 0
+        added = 0
+        finished = 0
         for i in range(PAIRS):
             a, b = 2 * i + 1, 2 * i + 2
             now = [j for j in (a, b) if j < TILES]
             for j in now:
                 turn_down(j)
-            for j in now:
                 turn_up(j)
+            ready = carried
             if i == 0:
-                if PA[0] != "n":
-                    part(a + 2, PA[0])
+                part(a + 2, "v")
                 quantize_h(last)
-            else:
-                carry_all(a - 2)
-                if i > 1:
-                    add_all(a - 4)
-                add_all(a - 3)
-                quantize_inc(a - 1)
-            carry_all(a - 1)
-            for s in range(2):
-                for j in now:
-                    empty_inc(s, j, "s")
             if a + 2 < TILES:
-                if i > 0 and PA[i] != "n":
-                    part(a + 2, PA[i])
                 widen(a + 2)
-            if b + 2 < TILES:
-                if PB[i] != "n":
-                    part(b + 2, PB[i])
-                widen(b + 2)
-            if i > 1:
-                finish_all(a - 4)
             if i > 0:
-                finish_all(a - 3)
+                quantize_inc(a - 1)
             if b < TILES:
+                for j in range(carried, carried + COUNTS[i]):
+                    carry_all(j)
+                carried = carried + COUNTS[i]
+            empty_inc(0, a, "s")
+            empty_inc(1, a, "s")
+            if b + 2 < TILES:
+                widen(b + 2)
+            for j in (a + 2, b + 2):
+                if j < TILES and i > 0 and PENG[j] != "n":
+                    part(j, PENG[j])
+            if b < TILES:
+                empty_inc(0, b, "s")
+                empty_inc(1, b, "s")
+                for j in range(added, ready):
+                    add_all(j)
+                added = ready
                 quantize_inc(a)
-            else:
+                for j in range(finished, min(added, finished + SILUS[i])):
+                    finish_all(j)
+                    finished = j + 1
+        for j in range(carried, TILES):
+            if j - 4 >= added:
+                add_all(added)
+                added = added + 1
+            if j == TILES - 1 - QLAST:
                 for s in range(2):
-                    quantize_inc(a, s, 1)
-        carry_all(TILES - 1)
-        for j in (TILES - 3, TILES - 2, TILES - 1):
-            for lo, width in parts(j):
-                add_edge(j, lo, width)
-                finish(j, lo, width)
+                    quantize_inc(TILES - 1, s, 1)
+            carry_all(j)
+            if added < j:
+                add_all(added)
+                added = added + 1
+        for j in range(added, TILES):
+            add_all(j)
+        for j in range(finished, TILES):
+            finish_all(j)

@@ -20,14 +20,9 @@ TILES = NE // P
 PAIRS = TILES // 2
 CHUNKS = 4
 FLOPS = 2 * 2 * NV * C * F + 2 * 2 * NE * NV * F
-TURNED_BANKS = 4
-WARM = 3
 X_PIECES = (((0, 2), (2, 2)), ((0, 2), (2, 2)), ((0, 4),), ((0, 4),))
-H3 = "sssv"
-PENG = "nnnnnnsnsnsv"
-COUNTS = (1,2,1,2,1)
-SILUS = (0,1,2,2,2)
-QLAST = 2
+RUNS = ((1, 2, 3), (4, 5, 6), (7, 8, 9), (10, 11))
+HALVED = 9
 HALVED = 9
 LAST = ((0, 256), (256, 128), (384, 128))
 
@@ -39,8 +34,7 @@ def tile_simplicialboundarycoboundarymessage_d1p_kernel(
     with ExitStack() as ctx:
         keep = ctx.enter_context(tc.tile_pool(name="keep", bufs=1))
         work = ctx.enter_context(tc.tile_pool(name="work", bufs=3))
-        turned = ctx.enter_context(tc.psum_pool(name="turned", bufs=TURNED_BANKS))
-        sums = ctx.enter_context(tc.psum_pool(name="sums", bufs=8 - TURNED_BANKS))
+        banks = ctx.enter_context(tc.psum_pool(name="banks", bufs=8))
         ctx.enter_context(tc.manual_schedule())
 
         ident = keep.tile([P, P], F32, name="ident")
@@ -122,7 +116,7 @@ def tile_simplicialboundarycoboundarymessage_d1p_kernel(
         nc.scalar.activation(out=warm[:], in_=warm[:], func=SILU)
 
         def warm_up(n):
-            bank = sums.tile([P, F], F32, name="acc")
+            bank = banks.tile([P, F], F32, name="bank")
             for k in range(n):
                 nc.tensor.matmul(bank[:], lhsT=idle[:, :P], rhs=idle[:], start=True, stop=True)
 
@@ -139,7 +133,7 @@ def tile_simplicialboundarycoboundarymessage_d1p_kernel(
         x_planes = {}
 
         def turn_x(c, lo, n):
-            bank = turned.tile([P, 2, 128 * n], F32, name="bank")
+            bank = banks.tile([P, 2, 128 * n], F32, name="bank")
             for t in range(n):
                 words = x_slot(c, lo + t).bitcast(F32)
                 for u in range(2):
@@ -172,7 +166,7 @@ def tile_simplicialboundarycoboundarymessage_d1p_kernel(
             s = c // 2
             for f in range(4):
                 cols = slice(128 * f, 128 * f + 128)
-                bank = sums.tile([P, 4, 128], F32, name="acc")
+                bank = banks.tile([P, 4, 128], F32, name="bank")
                 for t in range(4):
                     rows = slice(128 * t, 128 * t + 128)
                     nc.tensor.matmul_mx(
@@ -202,7 +196,7 @@ def tile_simplicialboundarycoboundarymessage_d1p_kernel(
         parted = {}
 
         def widen(j):
-            tile = work.tile([P, 2, 2, 128, 2], BF16, name="wide", bufs=4)
+            tile = work.tile([P, 2, 2, 128, 2], BF16, name="wide", bufs=6)
             raw = up_raw[j // 2]
             for b in range(8):
                 g, q = divmod(b, 4)
@@ -228,7 +222,7 @@ def tile_simplicialboundarycoboundarymessage_d1p_kernel(
 
         def turn_down(j):
             words = down_raw[j // 2][:, j % 2, :].bitcast(F32)
-            bank = turned.tile([P, 2, 256], F32, name="bank")
+            bank = banks.tile([P, 2, 256], F32, name="bank")
             for g in range(2):
                 for u in range(2):
                     source = parted[j][:, g, u, :] if j in parted else words[:, 256 * g + u : 256 * g + 256 : 2]
@@ -237,7 +231,7 @@ def tile_simplicialboundarycoboundarymessage_d1p_kernel(
 
         def turn_up(j):
             words = wide[j][:].rearrange("m g u p e -> m (g u p e)").bitcast(F32)
-            bank = turned.tile([P, 2, 256], F32, name="bank")
+            bank = banks.tile([P, 2, 256], F32, name="bank")
             for g in range(2):
                 for u in range(2):
                     lo = 256 * g + 128 * u
@@ -246,7 +240,7 @@ def tile_simplicialboundarycoboundarymessage_d1p_kernel(
 
         def empty_inc(s, j, engine):
             if j not in i_grouped:
-                i_grouped[j] = work.tile([P, 2048], BF16, name="i_grouped", bufs=4, align_bytes=256)
+                i_grouped[j] = work.tile([P, 2048], BF16, name="i_grouped", bufs=6, align_bytes=256)
             view = i_grouped[j][:, 1024 * s : 1024 * s + 1024].bitcast(F32).rearrange("p (x u) -> p x u", u=2)
             move(engine, view, i_turned[s, j][:].rearrange("p u x -> p x u"))
 
@@ -265,10 +259,7 @@ def tile_simplicialboundarycoboundarymessage_d1p_kernel(
 
         def carry(j, lo=0, width=F):
             cols = slice(lo, lo + width)
-            if j == TILES - 1:
-                bank = turned.tile([P, width], F32, name="bank")
-            else:
-                bank = sums.tile([P, width], F32, name="acc")
+            bank = banks.tile([P, width], F32, name="bank")
             for c in range(CHUNKS):
                 rows = slice(128 * c, 128 * c + 128)
                 nc.tensor.matmul_mx(
@@ -295,13 +286,33 @@ def tile_simplicialboundarycoboundarymessage_d1p_kernel(
             nc.sync.dma_start(out=out_rows[:, j, lo : lo + width], in_=result[:])
 
         def parts(j):
-            if j == TILES - 1:
-                return LAST
             return ((0, 256), (256, 256)) if j >= HALVED else ((0, F),)
 
-        warm_up(WARM)
-        first = ((0, 2), (2, 1), (3, 1))
-        for lo, n in first:
+        def turn(j):
+            turn_down(j)
+            turn_up(j)
+
+        def empty(j):
+            empty_inc(0, j, "s")
+            empty_inc(1, j, "s")
+
+        def carry_all(j):
+            if j >= 0:
+                for lo, width in parts(j):
+                    carry(j, lo, width)
+
+        def add_all(j):
+            if j >= 0:
+                for lo, width in parts(j):
+                    add_edge(j, lo, width)
+
+        def finish_all(j):
+            if j >= 0:
+                for lo, width in parts(j):
+                    finish(j, lo, width)
+
+        warm_up(3)
+        for lo, n in ((0, 2), (2, 1), (3, 1)):
             turn_x(0, lo, n)
         empty_x(0, 0, 2, "v")
         empty_x(0, 2, 1, "s")
@@ -310,93 +321,73 @@ def tile_simplicialboundarycoboundarymessage_d1p_kernel(
         quantize_x(0, 2, 1)
         quantize_x(0, 3, 1)
         warm_up(2)
-        for c in range(CHUNKS - 1):
+        last = CHUNKS - 1
+        for c in range(last):
             turn_x(c + 1, 0, 2)
             turn_x(c + 1, 2, 2)
             empty_x(c + 1, 0, 2, "s")
             empty_x(c + 1, 2, 2, "v")
             project(c)
             for f in range(4):
-                if c == 0 and f == 1:
-                    empty_h(c, f, "v")
-                else:
-                    empty_h(c, f, "s")
+                empty_h(c, f, "v" if (c, f) == (0, 1) else "s")
             if c > 0:
                 quantize_h(c - 1)
             quantize_x(c + 1)
             widen(c)
-        last = CHUNKS - 1
-        turn_down(0)
-        turn_up(0)
+        turn(0)
         project(last)
         empty_inc(1, 0, "v")
         empty_inc(0, 0, "s")
+        widen(RUNS[0][-1])
         quantize_h(last - 1)
-        quantize_inc(0)
         for f in range(4):
-            empty_h(last, f, H3[f])
-        def carry_all(j):
-            for lo, width in parts(j):
-                carry(j, lo, width)
+            empty_h(last, f, "v" if f == 3 else "s")
+        quantize_inc(0)
 
-        def add_all(j):
-            for lo, width in parts(j):
-                add_edge(j, lo, width)
-
-        def finish_all(j):
-            for lo, width in parts(j):
-                finish(j, lo, width)
-
-        carried = 0
-        added = 0
-        finished = 0
-        for i in range(PAIRS):
-            a, b = 2 * i + 1, 2 * i + 2
-            now = [j for j in (a, b) if j < TILES]
-            for j in now:
-                turn_down(j)
-                turn_up(j)
-            ready = carried
-            if i == 0:
-                part(a + 2, "v")
+        for run, coming in zip(RUNS[:-1], RUNS[1:]):
+            a = run[0]
+            for j in run:
+                turn(j)
+            if run is RUNS[0]:
                 quantize_h(last)
-            if a + 2 < TILES:
-                widen(a + 2)
-            if i > 0:
+                part(coming[0], "v")
+            else:
                 quantize_inc(a - 1)
-            if b < TILES:
-                for j in range(carried, carried + COUNTS[i]):
-                    carry_all(j)
-                carried = carried + COUNTS[i]
-            empty_inc(0, a, "s")
-            empty_inc(1, a, "s")
-            if b + 2 < TILES:
-                widen(b + 2)
-            for j in (a + 2, b + 2):
-                if j < TILES and i > 0 and PENG[j] != "n":
-                    part(j, PENG[j])
-            if b < TILES:
-                empty_inc(0, b, "s")
-                empty_inc(1, b, "s")
-                for j in range(added, ready):
-                    add_all(j)
-                added = ready
-                quantize_inc(a)
-                for j in range(finished, min(added, finished + SILUS[i])):
-                    finish_all(j)
-                    finished = j + 1
-        for j in range(carried, TILES):
-            if j - 4 >= added:
-                add_all(added)
-                added = added + 1
-            if j == TILES - 1 - QLAST:
-                for s in range(2):
-                    quantize_inc(TILES - 1, s, 1)
-            carry_all(j)
-            if added < j:
-                add_all(added)
-                added = added + 1
-        for j in range(added, TILES):
+                add_all(a - 3)
+            empty(a)
+            quantize_inc(a)
+            for j in (a - 2, a - 1, a):
+                carry_all(j)
+            empty(a + 1)
+            empty(a + 2)
+            widen(coming[0])
+            add_all(a - 2)
+            for j in coming[1:]:
+                widen(j)
+            finish_all(a - 4)
+            part(coming[1], "s")
+            finish_all(a - 3)
+            for j in coming[2:]:
+                part(j, "s" if run is RUNS[0] else "v")
+            add_all(a - 1)
+            quantize_inc(a + 1)
+            finish_all(a - 2)
+        a, b = RUNS[-1]
+        turn(a)
+        turn(b)
+        quantize_inc(a - 1)
+        add_all(a - 3)
+        finish_all(a - 4)
+        empty(a)
+        quantize_inc(a)
+        carry_all(a - 2)
+        carry_all(a - 1)
+        empty(b)
+        add_all(a - 2)
+        quantize_inc(b)
+        carry_all(a)
+        carry_all(b)
+        for j in (a - 1, a, b):
             add_all(j)
-        for j in range(finished, TILES):
+        for j in range(a - 3, TILES):
             finish_all(j)

@@ -21,6 +21,8 @@ PAIRS = TILES // 2
 CHUNKS = 4
 FLOPS = 2 * 2 * NV * C * F + 2 * 2 * NE * NV * F
 X_PIECES = (((0, 2), (2, 2)), ((0, 2), (2, 2)), ((0, 4),), ((0, 4),))
+W_PIECES = (((0, 4),), ((0, 4),))
+UP_PIECES = ((0, 2), (2, 2), (4, 2), (6, 2), (8, 2), (10, 2))
 RUNS = ((1, 2, 3), (4, 5, 6), (7, 8, 9), (10, 11))
 HALVED = 9
 HALVED = 9
@@ -51,9 +53,18 @@ def tile_simplicialboundarycoboundarymessage_d1p_kernel(
                 piece = keep.tile([P, n, C], BF16, name="x_raw%d_%d" % (c, lo))
                 for t in range(n):
                     x_raw[c, lo + t] = (piece, t)
-        w_codes = [keep.tile([P, F], U32, name="w_codes%d" % s, align_bytes=256) for s in range(2)]
+        w_codes = {}
+        for s in range(2):
+            for lo, n in W_PIECES[s]:
+                piece = keep.tile([P, 128 * n], U32, name="w_codes%d_%d" % (s, lo), align_bytes=256)
+                for f in range(n):
+                    w_codes[s, lo + f] = (piece, f)
         down_raw = [keep.tile([P, 2, NV], BF16, name="down_raw%d" % i) for i in range(PAIRS)]
-        up_raw = [keep.tile([P, 2, NV], U8, name="up_raw%d" % i) for i in range(PAIRS)]
+        up_raw = {}
+        for lo, n in UP_PIECES:
+            piece = keep.tile([P, n, NV], U8, name="up_raw%d" % lo)
+            for t in range(n):
+                up_raw[lo + t] = (piece, t)
         edge = [keep.tile([P, 4, F], BF16, name="edge%d" % i) for i in range(3)]
         down_rows = inc_down.rearrange("(m j) k -> m j k", j=TILES)
         up_rows = inc_up_bytes.rearrange("(m j) k -> m j k", j=TILES)
@@ -73,7 +84,8 @@ def tile_simplicialboundarycoboundarymessage_d1p_kernel(
 
         def load_w(s):
             words = (w0_words, w2_words)[s][0].rearrange("p n t -> p (n t)").bitcast(I32)
-            nc.sync.dma_start(out=w_codes[s][:].bitcast(I32), in_=words)
+            for lo, n in W_PIECES[s]:
+                nc.sync.dma_start(out=w_codes[s, lo][0][:].bitcast(I32), in_=words[:, 128 * lo : 128 * (lo + n)])
 
         def load_planes(s, queue):
             for q in range(4):
@@ -88,8 +100,8 @@ def tile_simplicialboundarycoboundarymessage_d1p_kernel(
         def load_down(i):
             nc.sync.dma_start(out=down_raw[i][:], in_=down_rows[:, 2 * i : 2 * i + 2, :])
 
-        def load_up(i):
-            nc.sync.dma_start(out=up_raw[i][:], in_=up_rows[:, 2 * i : 2 * i + 2, :])
+        def load_up(lo, n):
+            nc.sync.dma_start(out=up_raw[lo][0][:], in_=up_rows[:, lo : lo + n, :])
 
         def load_edge(i):
             nc.sync.dma_start(out=edge[i][:], in_=x1_rows[:, 4 * i : 4 * i + 4, :])
@@ -100,16 +112,24 @@ def tile_simplicialboundarycoboundarymessage_d1p_kernel(
         load_w(0)
         load_x(2)
         load_scale(nc.sync)
-        load_up(0)
+        load_up(0, 2)
         load_x(3)
         load_planes(1, nc.sync)
         load_w(1)
-        for i in range(PAIRS):
-            load_down(i)
-            if i + 1 < PAIRS:
-                load_up(i + 1)
-            if i % 2 == 1:
-                load_edge(i // 2)
+        load_down(0)
+        load_up(2, 2)
+        load_down(1)
+        load_down(2)
+        load_up(4, 2)
+        load_up(6, 2)
+        load_down(3)
+        load_edge(0)
+        load_up(8, 2)
+        load_down(4)
+        load_edge(1)
+        load_up(10, 2)
+        load_down(5)
+        load_edge(2)
 
         warm = keep.tile([P, 1], F32, name="warm")
         nc.vector.memset(warm[:], 0.0)
@@ -166,6 +186,7 @@ def tile_simplicialboundarycoboundarymessage_d1p_kernel(
             s = c // 2
             for f in range(4):
                 cols = slice(128 * f, 128 * f + 128)
+                w_piece, w_block = w_codes[s, f]
                 bank = banks.tile([P, 4, 128], F32, name="bank")
                 for t in range(4):
                     rows = slice(128 * t, 128 * t + 128)
@@ -173,7 +194,7 @@ def tile_simplicialboundarycoboundarymessage_d1p_kernel(
                         out=bank[:, t, :],
                         lhsT=x_codes[c][:, rows].bitcast(FP8X4),
                         lhsT_scale=x_planes[c][:, rows],
-                        rhs=w_codes[s][:, cols].bitcast(FP8X4),
+                        rhs=w_piece[:, 128 * w_block : 128 * w_block + 128].bitcast(FP8X4),
                         rhs_scale=w_scales[:, s, cols],
                         start=True,
                         stop=True,
@@ -197,12 +218,12 @@ def tile_simplicialboundarycoboundarymessage_d1p_kernel(
 
         def widen(j):
             tile = work.tile([P, 2, 2, 128, 2], BF16, name="wide", bufs=6)
-            raw = up_raw[j // 2]
+            raw, row = up_raw[j]
             for b in range(8):
                 g, q = divmod(b, 4)
                 nc.vector.tensor_scalar(
                     out=tile[:, g, :, 32 * q : 32 * q + 32, :].rearrange("m u p e -> m p u e"),
-                    in0=raw[:, j % 2, 128 * b : 128 * b + 128].bitcast(FP8).rearrange("m (p u e) -> m p u e", u=2, e=2),
+                    in0=raw[:, row, 128 * b : 128 * b + 128].bitcast(FP8).rearrange("m (p u e) -> m p u e", u=2, e=2),
                     scalar1=up_scale[:, j, b : b + 1],
                     scalar2=None,
                     op0=MULT,
@@ -283,7 +304,8 @@ def tile_simplicialboundarycoboundarymessage_d1p_kernel(
         def finish(j, lo=0, width=F):
             result = keep.tile([P, width], F32, name="result%d_%d" % (j, lo))
             nc.scalar.activation(out=result[:], in_=z_tiles[j, lo][:], func=SILU)
-            nc.sync.dma_start(out=out_rows[:, j, lo : lo + width], in_=result[:])
+            queue = nc.scalar if (j, lo + width) == (TILES - 1, F) else nc.sync
+            queue.dma_start(out=out_rows[:, j, lo : lo + width], in_=result[:])
 
         def parts(j):
             return ((0, 256), (256, 256)) if j >= HALVED else ((0, F),)
@@ -328,11 +350,14 @@ def tile_simplicialboundarycoboundarymessage_d1p_kernel(
             empty_x(c + 1, 0, 2, "s")
             empty_x(c + 1, 2, 2, "v")
             project(c)
+            if c == 0:
+                quantize_x(1, 0, 2)
+                quantize_x(1, 2, 2)
             for f in range(4):
                 empty_h(c, f, "v" if (c, f) == (0, 1) else "s")
             if c > 0:
                 quantize_h(c - 1)
-            quantize_x(c + 1)
+                quantize_x(c + 1)
             widen(c)
         turn(0)
         project(last)
@@ -350,12 +375,16 @@ def tile_simplicialboundarycoboundarymessage_d1p_kernel(
                 turn(j)
             if run is RUNS[0]:
                 quantize_h(last)
+                empty_inc(0, a, "s")
+                quantize_inc(a, 0, 1)
                 part(coming[0], "v")
+                empty_inc(1, a, "s")
+                quantize_inc(a, 1, 1)
             else:
                 quantize_inc(a - 1)
                 add_all(a - 3)
-            empty(a)
-            quantize_inc(a)
+                empty(a)
+                quantize_inc(a)
             for j in (a - 2, a - 1, a):
                 carry_all(j)
             empty(a + 1)
@@ -364,11 +393,13 @@ def tile_simplicialboundarycoboundarymessage_d1p_kernel(
             add_all(a - 2)
             for j in coming[1:]:
                 widen(j)
+            if run is RUNS[1]:
+                part(coming[0], "s")
             finish_all(a - 4)
             part(coming[1], "s")
             finish_all(a - 3)
-            for j in coming[2:]:
-                part(j, "s" if run is RUNS[0] else "v")
+            if run is RUNS[0]:
+                part(coming[2], "s")
             add_all(a - 1)
             quantize_inc(a + 1)
             finish_all(a - 2)
@@ -378,11 +409,13 @@ def tile_simplicialboundarycoboundarymessage_d1p_kernel(
         quantize_inc(a - 1)
         add_all(a - 3)
         finish_all(a - 4)
-        empty(a)
-        quantize_inc(a)
+        empty_inc(0, a, "s")
+        empty_inc(1, a, "v")
+        empty(b)
+        quantize_inc(a, 0, 1)
+        quantize_inc(a, 1, 1)
         carry_all(a - 2)
         carry_all(a - 1)
-        empty(b)
         add_all(a - 2)
         quantize_inc(b)
         carry_all(a)

@@ -25,8 +25,6 @@ W_PIECES = (((0, 4),), ((0, 4),))
 UP_PIECES = ((0, 2), (2, 2), (4, 2), (6, 2), (8, 2), (10, 2))
 RUNS = ((1, 2, 3), (4, 5, 6), (7, 8, 9), (10, 11))
 HALVED = 9
-HALVED = 9
-LAST = ((0, 256), (256, 128), (384, 128))
 
 
 def tile_simplicialboundarycoboundarymessage_d1p_kernel(
@@ -301,11 +299,17 @@ def tile_simplicialboundarycoboundarymessage_d1p_kernel(
             nc.vector.tensor_tensor(out=z[:], in0=z_sums[j, lo][:], in1=edge[j // 4][:, j % 4, lo : lo + width], op=ADD)
             z_tiles[j, lo] = z
 
+        results = {}
+
         def finish(j, lo=0, width=F):
-            result = keep.tile([P, width], F32, name="result%d_%d" % (j, lo))
-            nc.scalar.activation(out=result[:], in_=z_tiles[j, lo][:], func=SILU)
-            queue = nc.scalar if (j, lo + width) == (TILES - 1, F) else nc.sync
-            queue.dma_start(out=out_rows[:, j, lo : lo + width], in_=result[:])
+            if lo == 0:
+                results[j] = keep.tile([P, F], F32, name="result%d" % j)
+            nc.scalar.activation(out=results[j][:, lo : lo + width], in_=z_tiles[j, lo][:], func=SILU)
+            if j == TILES - 1:
+                queue = nc.scalar if lo + width == F else nc.sync
+                queue.dma_start(out=out_rows[:, j, lo : lo + width], in_=results[j][:, lo : lo + width])
+            elif lo + width == F:
+                nc.sync.dma_start(out=out_rows[:, j, :], in_=results[j][:])
 
         def parts(j):
             return ((0, 256), (256, 256)) if j >= HALVED else ((0, F),)
@@ -342,7 +346,7 @@ def tile_simplicialboundarycoboundarymessage_d1p_kernel(
         empty_x(0, 3, 1, "s")
         quantize_x(0, 2, 1)
         quantize_x(0, 3, 1)
-        warm_up(2)
+        warm_up(1)
         last = CHUNKS - 1
         for c in range(last):
             turn_x(c + 1, 0, 2)
@@ -377,7 +381,6 @@ def tile_simplicialboundarycoboundarymessage_d1p_kernel(
                 quantize_h(last)
                 empty_inc(0, a, "s")
                 quantize_inc(a, 0, 1)
-                part(coming[0], "v")
                 empty_inc(1, a, "s")
                 quantize_inc(a, 1, 1)
             else:

from contextlib import ExitStack

import concourse.mybir as mybir
from concourse.masks import make_identity

F32 = mybir.dt.float32
BF16 = mybir.dt.bfloat16
U32 = mybir.dt.uint32
I32 = mybir.dt.int32
U8 = mybir.dt.uint8
FP8 = mybir.dt.float8_e4m3fn
FP8X4 = mybir.dt.float8_e4m3fn_x4
ADD = mybir.AluOpType.add
MULT = mybir.AluOpType.mult
SILU = mybir.ActivationFunctionType.Silu

P = 128
NE, NV, C, F = 1536, 1024, 512, 512
TILES = NE // P
PAIRS = TILES // 2
CHUNKS = 4
FLOPS = 2 * 2 * NV * C * F + 2 * 2 * NE * NV * F
X_PIECES = (((0, 2), (2, 2)), ((0, 2), (2, 2)), ((0, 4),), ((0, 4),))
W_PIECES = (((0, 4),), ((0, 4),))
UP_PIECES = ((0, 2), (2, 2), (4, 2), (6, 2), (8, 2), (10, 2))
RUNS = ((1, 2, 3), (4, 5, 6), (7, 8, 9), (10, 11))
HALVED = 9


def tile_simplicialboundarycoboundarymessage_d1p_kernel(
    tc, x0, x1, x2, inc_down, inc_up_bytes, inc_up_scale, w0_words, w0_scales, w2_words, w2_scales, out
):
    nc = tc.nc
    with ExitStack() as ctx:
        keep = ctx.enter_context(tc.tile_pool(name="keep", bufs=1))
        work = ctx.enter_context(tc.tile_pool(name="work", bufs=3))
        banks = ctx.enter_context(tc.psum_pool(name="banks", bufs=8))
        ctx.enter_context(tc.manual_schedule())

        ident = keep.tile([P, P], F32, name="ident")
        make_identity(nc, ident[:])
        idle = keep.tile([P, F], BF16, name="idle")
        nc.vector.memset(idle[:], 0.0)
        w_scales = keep.tile([P, 2, F], U8, name="w_scales", align_bytes=256)
        nc.vector.memset(w_scales[:].rearrange("p s n -> p (s n)").bitcast(I32), 0)
        up_scale = keep.tile([P, TILES, 8], F32, name="up_scale")

        x_raw = {}
        for c in range(CHUNKS):
            for lo, n in X_PIECES[c]:
                piece = keep.tile([P, n, C], BF16, name="x_raw%d_%d" % (c, lo))
                for t in range(n):
                    x_raw[c, lo + t] = (piece, t)
        w_codes = {}
        for s in range(2):
            for lo, n in W_PIECES[s]:
                piece = keep.tile([P, 128 * n], U32, name="w_codes%d_%d" % (s, lo), align_bytes=256)
                for f in range(n):
                    w_codes[s, lo + f] = (piece, f)
        down_raw = [keep.tile([P, 2, NV], BF16, name="down_raw%d" % i) for i in range(PAIRS)]
        up_raw = {}
        for lo, n in UP_PIECES:
            piece = keep.tile([P, n, NV], U8, name="up_raw%d" % lo)
            for t in range(n):
                up_raw[lo + t] = (piece, t)
        edge = [keep.tile([P, 4, F], BF16, name="edge%d" % i) for i in range(3)]
        down_rows = inc_down.rearrange("(m j) k -> m j k", j=TILES)
        up_rows = inc_up_bytes.rearrange("(m j) k -> m j k", j=TILES)
        x1_rows = x1.rearrange("(m j) f -> m j f", j=TILES)
        out_rows = out.rearrange("(m j) f -> m j f", j=TILES)

        def x_rows(c):
            return (x0, x2)[c // 2].rearrange("(g m t) c -> g m t c", m=P, t=4)[c % 2]

        def x_slot(c, t):
            piece, row = x_raw[c, t]
            return piece[:, row, :]

        def load_x(c):
            for lo, n in X_PIECES[c]:
                nc.sync.dma_start(out=x_raw[c, lo][0][:], in_=x_rows(c)[:, lo : lo + n, :])

        def load_w(s):
            words = (w0_words, w2_words)[s][0].rearrange("p n t -> p (n t)").bitcast(I32)
            for lo, n in W_PIECES[s]:
                nc.sync.dma_start(out=w_codes[s, lo][0][:].bitcast(I32), in_=words[:, 128 * lo : 128 * (lo + n)])

        def load_planes(s, queue):
            for q in range(4):
                queue.dma_start(
                    out=w_scales[32 * q : 32 * q + 4, s, :].bitcast(I32),
                    in_=(w0_scales, w2_scales)[s][0, 4 * q : 4 * q + 4, :].bitcast(I32),
                )

        def load_scale(queue):
            queue.dma_start(out=up_scale[:], in_=inc_up_scale.rearrange("(m j) q -> m j q", j=TILES))

        def load_down(i):
            nc.sync.dma_start(out=down_raw[i][:], in_=down_rows[:, 2 * i : 2 * i + 2, :])

        def load_up(lo, n):
            nc.sync.dma_start(out=up_raw[lo][0][:], in_=up_rows[:, lo : lo + n, :])

        def load_edge(i):
            nc.sync.dma_start(out=edge[i][:], in_=x1_rows[:, 4 * i : 4 * i + 4, :])

        load_planes(0, nc.scalar)
        load_x(0)
        load_x(1)
        load_w(0)
        load_x(2)
        load_scale(nc.sync)
        load_up(0, 2)
        load_x(3)
        load_planes(1, nc.sync)
        load_w(1)
        load_down(0)
        load_up(2, 2)
        load_down(1)
        load_down(2)
        load_up(4, 2)
        load_up(6, 2)
        load_down(3)
        load_edge(0)
        load_up(8, 2)
        load_down(4)
        load_edge(1)
        load_up(10, 2)
        load_down(5)
        load_edge(2)

        warm = keep.tile([P, 1], F32, name="warm")
        nc.vector.memset(warm[:], 0.0)
        nc.scalar.activation(out=warm[:], in_=warm[:], func=SILU)

        def warm_up(n):
            bank = banks.tile([P, F], F32, name="bank")
            for k in range(n):
                nc.tensor.matmul(bank[:], lhsT=idle[:, :P], rhs=idle[:], start=True, stop=True)


        def move(engine, out_ap, in_ap):
            if engine == "v":
                nc.vector.tensor_copy(out=out_ap, in_=in_ap)
            else:
                nc.scalar.copy(out=out_ap, in_=in_ap)

        x_turned = {}
        x_grouped = {}
        x_codes = {}
        x_planes = {}

        def turn_x(c, lo, n):
            bank = banks.tile([P, 2, 128 * n], F32, name="bank")
            for t in range(n):
                words = x_slot(c, lo + t).bitcast(F32)
                for u in range(2):
                    nc.tensor.transpose(bank[:, u, 128 * t : 128 * t + 128], words[:, u:256:2], ident[:])
            x_turned[c, lo] = bank

        def empty_x(c, lo, n, engine):
            if lo == 0:
                x_grouped[c] = work.tile([P, 2048], BF16, name="x_grouped", align_bytes=256)
            view = x_grouped[c][:, 512 * lo : 512 * (lo + n)].bitcast(F32).rearrange("p (x u) -> p x u", u=2)
            move(engine, view, x_turned[c, lo][:].rearrange("p u x -> p x u"))

        def quantize_x(c, lo=0, n=4):
            if lo == 0:
                x_codes[c] = work.tile([P, 512], U32, name="x_codes", align_bytes=256)
                x_planes[c] = work.tile([P, 512], U8, name="x_planes", align_bytes=256)
            cols = slice(128 * lo, 128 * (lo + n))
            nc.vector.quantize_mx(
                out=x_codes[c][:, cols].bitcast(FP8X4),
                scales=x_planes[c][:, cols],
                in_=x_grouped[c][:, 512 * lo : 512 * (lo + n)],
            )

        h_sums = {}
        h_grouped = {}
        h_codes = {}
        h_planes = {}

        def project(c):
            s = c // 2
            for f in range(4):
                cols = slice(128 * f, 128 * f + 128)
                w_piece, w_block = w_codes[s, f]
                bank = banks.tile([P, 4, 128], F32, name="bank")
                for t in range(4):
                    rows = slice(128 * t, 128 * t + 128)
                    nc.tensor.matmul_mx(
                        out=bank[:, t, :],
                        lhsT=x_codes[c][:, rows].bitcast(FP8X4),
                        lhsT_scale=x_planes[c][:, rows],
                        rhs=w_piece[:, 128 * w_block : 128 * w_block + 128].bitcast(FP8X4),
                        rhs_scale=w_scales[:, s, cols],
                        start=True,
                        stop=True,
                    )
                h_sums[c, f] = bank

        def empty_h(c, f, engine):
            if f == 0:
                h_grouped[c] = work.tile([P, 512, 4], BF16, name="h_grouped", align_bytes=256)
            move(engine, h_grouped[c][:, 128 * f : 128 * f + 128, :], h_sums[c, f][:].rearrange("p t n -> p n t"))

        def quantize_h(c):
            h_codes[c] = keep.tile([P, 512], U32, name="h_codes%d" % c, align_bytes=256)
            h_planes[c] = keep.tile([P, 512], U8, name="h_planes%d" % c, align_bytes=256)
            nc.vector.quantize_mx(
                out=h_codes[c][:].bitcast(FP8X4), scales=h_planes[c][:], in_=h_grouped[c][:].rearrange("p n t -> p (n t)")
            )

        wide = {}
        parted = {}

        def widen(j):
            tile = work.tile([P, 2, 2, 128, 2], BF16, name="wide", bufs=6)
            raw, row = up_raw[j]
            for b in range(8):
                g, q = divmod(b, 4)
                nc.vector.tensor_scalar(
                    out=tile[:, g, :, 32 * q : 32 * q + 32, :].rearrange("m u p e -> m p u e"),
                    in0=raw[:, row, 128 * b : 128 * b + 128].bitcast(FP8).rearrange("m (p u e) -> m p u e", u=2, e=2),
                    scalar1=up_scale[:, j, b : b + 1],
                    scalar2=None,
                    op0=MULT,
                )
            wide[j] = tile

        def part(j, engine):
            tile = work.tile([P, 2, 2, 128], F32, name="parted", bufs=4)
            words = down_raw[j // 2][:, j % 2, :].bitcast(F32)
            move(engine, tile[:], words.rearrange("m (g p u) -> m g u p", g=2, u=2))
            parted[j] = tile

        i_turned = {}
        i_grouped = {}
        i_codes = {}
        i_planes = {}

        def turn_down(j):
            words = down_raw[j // 2][:, j % 2, :].bitcast(F32)
            bank = banks.tile([P, 2, 256], F32, name="bank")
            for g in range(2):
                for u in range(2):
                    source = parted[j][:, g, u, :] if j in parted else words[:, 256 * g + u : 256 * g + 256 : 2]
                    nc.tensor.transpose(bank[:, u, 128 * g : 128 * g + 128], source, ident[:])
            i_turned[0, j] = bank

        def turn_up(j):
            words = wide[j][:].rearrange("m g u p e -> m (g u p e)").bitcast(F32)
            bank = banks.tile([P, 2, 256], F32, name="bank")
            for g in range(2):
                for u in range(2):
                    lo = 256 * g + 128 * u
                    nc.tensor.transpose(bank[:, u, 128 * g : 128 * g + 128], words[:, lo : lo + 128], ident[:])
            i_turned[1, j] = bank

        def empty_inc(s, j, engine):
            if j not in i_grouped:
                i_grouped[j] = work.tile([P, 2048], BF16, name="i_grouped", bufs=6, align_bytes=256)
            view = i_grouped[j][:, 1024 * s : 1024 * s + 1024].bitcast(F32).rearrange("p (x u) -> p x u", u=2)
            move(engine, view, i_turned[s, j][:].rearrange("p u x -> p x u"))

        def quantize_inc(j, lo=0, n=2):
            if j not in i_codes:
                i_codes[j] = work.tile([P, 512], U32, name="i_codes", bufs=7, align_bytes=256)
                i_planes[j] = work.tile([P, 512], U8, name="i_planes", bufs=7, align_bytes=256)
            cols = slice(256 * lo, 256 * (lo + n))
            nc.vector.quantize_mx(
                out=i_codes[j][:, cols].bitcast(FP8X4),
                scales=i_planes[j][:, cols],
                in_=i_grouped[j][:, 1024 * lo : 1024 * (lo + n)],
            )

        z_sums = {}

        def carry(j, lo=0, width=F):
            cols = slice(lo, lo + width)
            bank = banks.tile([P, width], F32, name="bank")
            for c in range(CHUNKS):
                rows = slice(128 * c, 128 * c + 128)
                nc.tensor.matmul_mx(
                    out=bank[:],
                    lhsT=i_codes[j][:, rows].bitcast(FP8X4),
                    lhsT_scale=i_planes[j][:, rows],
                    rhs=h_codes[c][:, cols].bitcast(FP8X4),
                    rhs_scale=h_planes[c][:, cols],
                    start=(c == 0),
                    stop=(c == CHUNKS - 1),
                )
            z_sums[j, lo] = bank

        z_tiles = {}

        def add_edge(j, lo=0, width=F):
            z = work.tile([P, width], F32, name="z", bufs=12)
            nc.vector.tensor_tensor(out=z[:], in0=z_sums[j, lo][:], in1=edge[j // 4][:, j % 4, lo : lo + width], op=ADD)
            z_tiles[j, lo] = z

        results = {}

        def finish(j, lo=0, width=F):
            if lo == 0:
                results[j] = keep.tile([P, F], F32, name="result%d" % j)
            nc.scalar.activation(out=results[j][:, lo : lo + width], in_=z_tiles[j, lo][:], func=SILU)
            if j == TILES - 1:
                queue = nc.scalar if lo + width == F else nc.sync
                queue.dma_start(out=out_rows[:, j, lo : lo + width], in_=results[j][:, lo : lo + width])
            elif lo + width == F:
                nc.sync.dma_start(out=out_rows[:, j, :], in_=results[j][:])

        def parts(j):
            return ((0, 256), (256, 256)) if j >= HALVED else ((0, F),)

        def turn(j):
            turn_down(j)
            turn_up(j)

        def empty(j):
            empty_inc(0, j, "s")
            empty_inc(1, j, "s")

        def carry_all(j):
            if j >= 0:
                for lo, width in parts(j):
                    carry(j, lo, width)

        def add_all(j):
            if j >= 0:
                for lo, width in parts(j):
                    add_edge(j, lo, width)

        def finish_all(j):
            if j >= 0:
                for lo, width in parts(j):
                    finish(j, lo, width)

        warm_up(3)
        for lo, n in ((0, 2), (2, 1), (3, 1)):
            turn_x(0, lo, n)
        empty_x(0, 0, 2, "v")
        empty_x(0, 2, 1, "s")
        quantize_x(0, 0, 2)
        empty_x(0, 3, 1, "s")
        quantize_x(0, 2, 1)
        quantize_x(0, 3, 1)
        warm_up(1)
        last = CHUNKS - 1
        for c in range(last):
            turn_x(c + 1, 0, 2)
            turn_x(c + 1, 2, 2)
            empty_x(c + 1, 0, 2, "s")
            empty_x(c + 1, 2, 2, "v")
            project(c)
            if c == 0:
                quantize_x(1, 0, 2)
                quantize_x(1, 2, 2)
            for f in range(4):
                empty_h(c, f, "v" if (c, f) == (0, 1) else "s")
            if c > 0:
                quantize_h(c - 1)
                quantize_x(c + 1)
            widen(c)
        turn(0)
        project(last)
        empty_inc(1, 0, "v")
        empty_inc(0, 0, "s")
        widen(RUNS[0][-1])
        quantize_h(last - 1)
        for f in range(4):
            empty_h(last, f, "v" if f == 3 else "s")
        quantize_inc(0)

        for run, coming in zip(RUNS[:-1], RUNS[1:]):
            a = run[0]
            for j in run:
                turn(j)
            if run is RUNS[0]:
                quantize_h(last)
                empty_inc(0, a, "s")
                quantize_inc(a, 0, 1)
                empty_inc(1, a, "s")
                quantize_inc(a, 1, 1)
            else:
                quantize_inc(a - 1)
                add_all(a - 3)
                empty(a)
                quantize_inc(a)
            for j in (a - 2, a - 1, a):
                carry_all(j)
            empty(a + 1)
            empty(a + 2)
            widen(coming[0])
            add_all(a - 2)
            for j in coming[1:]:
                widen(j)
            if run is RUNS[1]:
                part(coming[0], "s")
            finish_all(a - 4)
            part(coming[1], "s")
            finish_all(a - 3)
            if run is RUNS[0]:
                part(coming[2], "s")
            add_all(a - 1)
            quantize_inc(a + 1)
            finish_all(a - 2)
        a, b = RUNS[-1]
        turn(a)
        turn(b)
        quantize_inc(a - 1)
        add_all(a - 3)
        finish_all(a - 4)
        empty_inc(0, a, "s")
        empty_inc(1, a, "v")
        empty(b)
        quantize_inc(a, 0, 1)
        quantize_inc(a, 1, 1)
        carry_all(a - 2)
        carry_all(a - 1)
        add_all(a - 2)
        quantize_inc(b)
        carry_all(a)
        carry_all(b)
        for j in (a - 1, a, b):
            add_all(j)
        for j in range(a - 3, TILES):
            finish_all(j)
